import numpy as np
import ml_dtypes


def mxq(x, axis, fmt="e4m3"):
    dtype, down = {"e4m3": (ml_dtypes.float8_e4m3fn, 7), "e5m2": (ml_dtypes.float8_e5m2, 14)}[fmt]
    v = np.moveaxis(np.asarray(x, np.float32).astype(ml_dtypes.bfloat16).astype(np.float64), axis, -1)
    blocks = v.reshape(v.shape[:-1] + (-1, 32))
    amax = np.abs(blocks).max(-1, keepdims=True)
    byte = np.maximum(np.where(amax > 0, np.frexp(amax)[1] - 1 + 127, 0) - down, 1)
    scale = np.exp2(byte - 127.0)
    codes = (blocks / scale).astype(np.float32).astype(dtype).astype(np.float64)
    return np.moveaxis((codes * scale).reshape(v.shape), -1, axis)


WIDE = False


def mx_kscale(k):
    if not WIDE:
        return np.ones(k)
    levels = np.array([10, -10, 5, -5, 0])
    if k % 512:
        return np.exp2(np.random.permutation(np.resize(levels, k // 32))).repeat(32)
    a = np.empty((k // 512, 16))
    for p in range(k // 512):
        a[p, :8] = np.random.permutation(np.resize(levels, 8))
        for g in range(8):
            far = levels[np.abs(levels - a[p, g]) >= 10]
            a[p, g + 8] = far[np.random.randint(len(far))]
    return np.exp2(a.ravel()).repeat(32)


def f64(x):
    return np.asarray(x).astype(np.float64)


def striped(idx):
    return np.tile(idx.reshape(-1, 16).T, (8, 1)).astype(np.uint16)


def unstriped(offs):
    return offs[:16].T.reshape(-1).astype(np.int64)


E2M1 = np.array([0.0, 0.5, 1.0, 1.5, 2.0, 3.0, 4.0, 6.0, -0.0, -0.5, -1.0, -1.5, -2.0, -3.0, -4.0, -6.0])


def pack_weight(w, fmt):
    k, n = w.shape
    w = f64(np.asarray(w, np.float32).astype(ml_dtypes.bfloat16)).reshape(k // 32, 32, n)
    amax = np.abs(w).max(1)
    if fmt == "e4m3":
        byte = np.frexp(amax)[1] - 1 + 127 - 7
    else:
        mant, ex = np.frexp(amax / 6.0)
        byte = np.where(mant > 0.5, ex, ex - 1) + 127
    byte = np.clip(np.where(amax > 0, byte, 1), 1, 254)
    scaled = (w * np.exp2(127.0 - byte)[:, None, :]).reshape(k, n).astype(np.float32)
    by_word = np.ascontiguousarray(scaled.reshape(k // 512, 128, 4, n).transpose(0, 1, 3, 2))
    if fmt == "e4m3":
        words = by_word.astype(ml_dtypes.float8_e4m3fn).view(np.uint8)
    else:
        c = by_word.astype(ml_dtypes.float4_e2m1fn).view(np.uint8) & 0xF
        words = (c[..., 0::2] | (c[..., 1::2] << 4)).reshape(k // 512, 128, 2 * n)
    return np.ascontiguousarray(words), np.ascontiguousarray(byte.astype(np.uint8).reshape(k // 512, 16, n))


def unpack_weight(words, scales, fmt):
    g, _, n = scales.shape
    words = np.ascontiguousarray(words).reshape(g, 128, n, -1)
    if fmt == "e4m3":
        vals = words.view(ml_dtypes.float8_e4m3fn).astype(np.float64)
    else:
        nib = np.empty((g, 128, n, 4), np.uint8)
        nib[..., 0::2] = words & 0xF
        nib[..., 1::2] = words >> 4
        vals = E2M1[nib]
    vals = vals * np.repeat(np.exp2(scales.astype(np.float64) - 127.0), 8, axis=1)[..., None]
    return vals.transpose(0, 1, 3, 2).reshape(g * 512, n)


def planes(y):
    n, m = y.shape
    v = y.astype(np.float32).astype(ml_dtypes.bfloat16).astype(np.float64).reshape(n // 32, 32, m)
    top = np.abs(v).max(1)
    byte = np.clip(np.where(top > 0, np.frexp(top)[1] - 1 + 127 - 7, 1), 1, 254)
    codes = (v * np.exp2(127.0 - byte)[:, None, :]).reshape(n, m).astype(np.float32).astype(ml_dtypes.float8_e4m3fn).view(np.uint8)
    words = codes.reshape(n // 512, 128, 4, m).transpose(0, 1, 3, 2)
    return np.ascontiguousarray(words), np.ascontiguousarray(byte.astype(np.uint8).reshape(n // 512, 16, m))


def relu(v):
    return np.maximum(v, 0.0)


K, T, E, C, H, N = 512, 512, 4, 256, 512, 512


def by_expert(wq, xq):
    return np.concatenate([wq[e].T @ xq[:, e * C:(e + 1) * C] for e in range(E)], axis=1)


def setup_inputs():
    n = np.random.standard_normal
    s = mx_kscale(K)
    u = mx_kscale(H)
    slot_token = np.concatenate([np.random.permutation(T)[:C] for e in range(E)])
    x = pack_weight(n((K, T)) * s[:, None], "e4m3")
    w = [pack_weight(m, "e2m1") for m in n((E, K, N)) / np.sqrt(K) / s[None, :, None]]
    wb = [pack_weight(m, "e4m3") for m in n((E, H, N)) / np.sqrt(H) / u[None, :, None]]
    return {
        "x_words": x[0],
        "x_scales": x[1],
        "w_words": np.stack([m[0] for m in w]),
        "w_scales": np.stack([m[1] for m in w]),
        "wa": (n((E, K, H)) / np.sqrt(K) / s[None, :, None] * u).astype(np.float32),
        "wb_words": np.stack([m[0] for m in wb]),
        "wb_scales": np.stack([m[1] for m in wb]),
        "offs": striped(slot_token),
    }


def reference(x_words, x_scales, w_words, w_scales, wa, wb_words, wb_scales, offs):
    w = np.stack([unpack_weight(w_words[e], w_scales[e], "e2m1") for e in range(E)])
    waq = mxq(f64(wa), 1, "e4m3")
    wb = np.stack([unpack_weight(wb_words[e], wb_scales[e], "e4m3") for e in range(E)])
    idx = unstriped(offs)
    xq = unpack_weight(x_words, x_scales, "e4m3")[:, idx]
    h = relu(by_expert(waq, xq))
    y = by_expert(w, xq) + by_expert(wb, mxq(h, 0, "e4m3"))
    out = y
    out_0 = out
    return (out_0,) + planes(out_0)

@@ -1,0 +1,251 @@
+from contextlib import ExitStack
+
+import concourse.mybir as mybir
+
+K, T, E, C, H, N = 512, 512, 4, 256, 512, 512
+FLOPS = 2 * E * C * (K * H + K * N + H * N)
+
+F32 = mybir.dt.float32
+BF16 = mybir.dt.bfloat16
+I32 = mybir.dt.int32
+U32 = mybir.dt.uint32
+U16 = mybir.dt.uint16
+U8 = mybir.dt.uint8
+FP8X4 = mybir.dt.float8_e4m3fn_x4
+FP4X4 = mybir.dt.float4_e2m1fn_x4
+RELU = mybir.ActivationFunctionType.Relu
+
+P = 128
+PACK = 4
+HALF = 128
+
+
+def tile_moe_elr_s_relu_kernel(tc, x_words, x_scales, w_words, w_scales, wa, wb_words, wb_scales, offs, out_0, out_1, out_2):
+    nc = tc.nc
+    with ExitStack() as ctx:
+        keep = ctx.enter_context(tc.tile_pool(name="keep", bufs=1))
+        psum_h = ctx.enter_context(tc.psum_pool(name="psum_h", bufs=4))
+        psum_y = ctx.enter_context(tc.psum_pool(name="psum_y", bufs=4))
+
+        def sbuf(name, shape, dtype, tag=None):
+            return keep.tile(shape, dtype, name=name, tag=tag or name, align_bytes=64)
+
+        offsets = keep.tile([P, E * C // 16], U16, name="offsets")
+        x_w = sbuf("x_w", [P, T], U32)
+        x_s = sbuf("x_s", [P, T], U8)
+        w_s_raw = sbuf("w_s_raw", [P, E * N], U8)
+        wb_s_raw = sbuf("wb_s_raw", [P, N], U8)
+        nc.vector.memset(x_s[:].bitcast(I32), 0)
+        nc.vector.memset(wb_s_raw[:].bitcast(I32), 0)
+        nc.vector.memset(w_s_raw[:].bitcast(I32), 0)
+
+        wa_raw = {}
+
+        def load_wa(e, parts):
+            width = H // parts
+            rows = wa[e].rearrange("(p j) c -> p j c", j=PACK)
+            for a in range(parts):
+                tile = sbuf("wa_raw%d_%d" % (e, a), [P, PACK, width], F32)
+                nc.sync.dma_start(out=tile[:], in_=rows[:, :, a * width:(a + 1) * width])
+                wa_raw[(e, a)] = tile
+
+        parts = [2, 1, 1, 1]
+        nc.sync.dma_start(offsets[:], offs)
+        nc.sync.dma_start(out=x_w[:].bitcast(I32), in_=x_words[0].rearrange("p t d -> p (t d)").bitcast(I32))
+        for q in range(4):
+            nc.scalar.dma_start(out=x_s[32 * q:32 * q + 4, :].bitcast(I32), in_=x_scales[0, 4 * q:4 * q + 4, :].bitcast(I32))
+        load_wa(0, parts[0])
+        load_wa(1, parts[1])
+        for q in range(4):
+            nc.sync.dma_start(
+                out=w_s_raw[32 * q:32 * q + 4, :].bitcast(I32).rearrange("r (e c) -> r e c", e=E),
+                in_=w_scales[:, 0, 4 * q:4 * q + 4, :].bitcast(I32).rearrange("e r c -> r e c"),
+            )
+        load_wa(2, parts[2])
+        load_wa(3, parts[3])
+        for q in range(4):
+            nc.sync.dma_start(out=wb_s_raw[32 * q:32 * q + 16, :].bitcast(I32), in_=wb_scales[:, 0, 4 * q:4 * q + 4, :].bitcast(I32))
+        w_raw = {}
+        wb_raw = {}
+
+        def load_packed():
+            packed = sbuf("packed", [P, E * (N // 2 + N)], I32, tag="wa_raw1_0")
+            nc.sync.dma_start(
+                out=packed[:, 0:E * N // 2].rearrange("p (e c) -> p e c", e=E),
+                in_=w_words[:, 0].bitcast(I32).rearrange("e p c -> p e c"),
+            )
+            for pair in range(E // 2):
+                first = E * N // 2 + pair * 2 * N
+                nc.sync.dma_start(
+                    out=packed[:, first:first + 2 * N].rearrange("p (e c) -> p e c", e=2),
+                    in_=wb_words[2 * pair:2 * pair + 2, 0].rearrange("e p n d -> p e (n d)").bitcast(I32),
+                )
+            for e in range(E):
+                w_raw[e] = packed[:, e * N // 2:(e + 1) * N // 2].bitcast(U16)
+                wb_raw[e] = packed[:, E * N // 2 + e * N:E * N // 2 + (e + 1) * N]
+
+        def deal(dst, src):
+            nc.vector.tensor_copy(
+                out=dst.rearrange("p (t m) -> p m t", t=PACK),
+                in_=src.rearrange("p (m t) -> p m t", t=PACK),
+            )
+
+        xg_w = {}
+        xg_s = {}
+
+        def gather(e):
+            part = offsets[:, e * C // 16:(e + 1) * C // 16]
+            xg_w[e] = sbuf("xg_w%d" % e, [P, C], U32)
+            xg_s[e] = sbuf("xg_s%d" % e, [P, C], U8)
+            nc.vector.tensor_copy(xg_w[e][:], x_w[:].indirect(part))
+            nc.vector.tensor_copy(xg_s[e][:], x_s[:].indirect(part))
+
+        wa_bf = {}
+
+        def round_wa(e):
+            wa_bf[e] = sbuf("wa_bf%d" % e, [P, PACK * H], BF16)
+            dst = wa_bf[e][:].rearrange("p (t m j) -> p m j t", t=PACK, j=PACK)
+            per = P // parts[e]
+            for a in range(parts[e]):
+                src = wa_raw[(e, a)][:].rearrange("p j (m t) -> p m j t", t=PACK)
+                nc.scalar.copy(out=dst[:, a * per:(a + 1) * per], in_=src)
+
+        wa_w = {}
+        wa_s = {}
+
+        def quantize_wa(e):
+            wa_w[e] = sbuf("wa_w%d" % e, [P, H], U32)
+            wa_s[e] = sbuf("wa_s%d" % e, [P, H], U8)
+            nc.vector.quantize_mx(out=wa_w[e][:].bitcast(FP8X4), scales=wa_s[e][:], in_=wa_bf[e][:])
+
+        halves = [slice(s * HALF, (s + 1) * HALF) for s in range(C // HALF)]
+        wide = [slice(s * HALF * PACK, (s + 1) * HALF * PACK) for s in range(C // HALF)]
+        h_acc = {}
+
+        def hidden(e):
+            for s, slots in enumerate(halves):
+                acc = psum_h.tile([P, PACK, HALF], F32, name="acc_h")
+                h_acc[(e, s)] = acc
+                for t in range(PACK):
+                    cols = slice(t * P, (t + 1) * P)
+                    nc.tensor.matmul_mx(
+                        out=acc[:, t, :],
+                        lhsT=wa_w[e][:, cols].bitcast(FP8X4), lhsT_scale=wa_s[e][:, cols],
+                        rhs=xg_w[e][:, slots].bitcast(FP8X4), rhs_scale=xg_s[e][:, slots],
+                        start=True, stop=True,
+                    )
+
+        h_bf = {}
+
+        def round_h(e):
+            h_bf[e] = sbuf("h_bf%d" % e, [P, PACK * C], BF16)
+            for s in range(C // HALF):
+                woven = h_bf[e][:, wide[s]].rearrange("p (u t) -> p u t", t=PACK)
+                sums = h_acc[(e, s)][:].rearrange("p t u -> p u t")
+                if e == 2:
+                    nc.scalar.activation(out=woven, in_=sums, func=RELU)
+                else:
+                    nc.vector.tensor_scalar_max(out=woven, in0=sums, scalar1=0.0)
+
+        h_w = {}
+        h_s = {}
+
+        def quantize_h(e):
+            h_w[e] = sbuf("h_w%d" % e, [P, C], U32)
+            h_s[e] = sbuf("h_s%d" % e, [P, C], U8)
+            for s, slots in enumerate(halves):
+                nc.vector.quantize_mx(out=h_w[e][:, slots].bitcast(FP8X4), scales=h_s[e][:, slots], in_=h_bf[e][:, wide[s]])
+
+        w_w = {}
+        w_s = {}
+        wb_w = {}
+        wb_s = {}
+
+        def deal_scales():
+            wb_s[0] = sbuf("wb_s", [P, N], U8, tag="wa_bf2")
+            deal(wb_s[0][:], wb_s_raw[:])
+            for e in range(E):
+                w_s[e] = sbuf("w_s%d" % e, [P, N], U8)
+                deal(w_s[e][:], w_s_raw[:, e * N:(e + 1) * N])
+
+        def deal_weights(e):
+            w_w[e] = sbuf("w_w%d" % e, [P, 2 * N], U8)
+            wb_w[e] = sbuf("wb_w%d" % e, [P, N], I32)
+            deal(w_w[e][:].bitcast(U16), w_raw[e])
+            deal(wb_w[e][:], wb_raw[e])
+
+        out_rows = out_0.rearrange("(p t) j -> p t j", t=PACK)
+        y_s = sbuf("y_s", [P, E * C], U8)
+
+        def result(e):
+            last = e == E - 1
+            y_f = sbuf("y_f%d" % e, [P, PACK, C], F32)
+            y_bf = sbuf("y_bf%d" % e, [P, PACK * C], BF16)
+            y_w = sbuf("y_w%d" % e, [P, C], U32)
+            for s, slots in enumerate(halves):
+                acc = psum_y.tile([P, PACK, HALF], F32, name="acc_y")
+                for t in range(PACK):
+                    cols = slice(t * P, (t + 1) * P)
+                    nc.tensor.matmul_mx(
+                        out=acc[:, t, :],
+                        lhsT=w_w[e][:, 2 * t * P:2 * (t + 1) * P].bitcast(FP4X4), lhsT_scale=w_s[e][:, cols],
+                        rhs=xg_w[e][:, slots].bitcast(FP8X4), rhs_scale=xg_s[e][:, slots],
+                        start=True, stop=False,
+                    )
+                    nc.tensor.matmul_mx(
+                        out=acc[:, t, :],
+                        lhsT=wb_w[e][:, cols].bitcast(FP8X4), lhsT_scale=wb_s[0][4 * e:P, cols],
+                        rhs=h_w[e][:, slots].bitcast(FP8X4), rhs_scale=h_s[e][:, slots],
+                        start=False, stop=True,
+                    )
+                woven = y_bf[:, wide[s]].rearrange("p (u t) -> p u t", t=PACK)
+                if last:
+                    nc.vector.tensor_copy(out=woven, in_=acc[:].rearrange("p t u -> p u t"))
+                    nc.scalar.copy(out=y_f[:, :, slots], in_=acc[:])
+                    nc.sync.dma_start(out=out_rows[:, :, e * C + s * HALF:e * C + (s + 1) * HALF], in_=y_f[:, :, slots])
+                    nc.vector.quantize_mx(
+                        out=y_w[:, slots].bitcast(FP8X4),
+                        scales=y_s[:, e * C + s * HALF:e * C + (s + 1) * HALF],
+                        in_=y_bf[:, wide[s]],
+                    )
+                elif s == 0 or e < 2:
+                    nc.scalar.copy(out=y_f[:, :, slots], in_=acc[:])
+                    nc.scalar.copy(out=woven, in_=acc[:].rearrange("p t u -> p u t"))
+                else:
+                    nc.scalar.copy(out=y_f[:, :, slots], in_=acc[:])
+                    nc.vector.tensor_copy(
+                        out=y_bf[:, wide[s]].rearrange("p (c i t) -> p c t i", i=4, t=PACK),
+                        in_=y_f[:, :, slots].rearrange("p t (c i) -> p c t i", i=4),
+                    )
+            if not last:
+                nc.sync.dma_start(out=out_rows[:, :, e * C:(e + 1) * C], in_=y_f[:])
+                nc.vector.quantize_mx(out=y_w[:].bitcast(FP8X4), scales=y_s[:, e * C:(e + 1) * C], in_=y_bf[:])
+            nc.sync.dma_start(
+                out=out_1[0, :, e * C:(e + 1) * C, :].rearrange("p j d -> p (j d)").bitcast(I32),
+                in_=y_w[:].bitcast(I32),
+            )
+
+        for e in range(E):
+            gather(e)
+        for e in range(E):
+            round_wa(e)
+            if e == 1:
+                load_packed()
+            quantize_wa(e)
+            hidden(e)
+            if e >= 1:
+                round_h(e - 1)
+                quantize_h(e - 1)
+        deal_scales()
+        deal_weights(0)
+        round_h(E - 1)
+        for e in range(E):
+            if e + 1 < E:
+                deal_weights(e + 1)
+            if e == 0:
+                quantize_h(E - 1)
+            result(e)
+
+        for q in range(4):
+            queue = nc.sync if q % 2 == 0 else nc.scalar
+            queue.dma_start(out=out_2[0, 4 * q:4 * q + 4, :].bitcast(I32), in_=y_s[32 * q:32 * q + 4, :].bitcast(I32))

@@ -36,8 +36,8 @@ def tile_moe_elr_s_relu_kernel(tc, x_words, x_scales, w_words, w_scales, wa, wb_
         w_s_raw = sbuf("w_s_raw", [P, E * N], U8)
         wb_s_raw = sbuf("wb_s_raw", [P, N], U8)
         nc.vector.memset(x_s[:].bitcast(I32), 0)
-        nc.vector.memset(wb_s_raw[:].bitcast(I32), 0)
         nc.vector.memset(w_s_raw[:].bitcast(I32), 0)
+        nc.vector.memset(wb_s_raw[:].bitcast(I32), 0)
 
         wa_raw = {}
 
@@ -49,7 +49,23 @@ def tile_moe_elr_s_relu_kernel(tc, x_words, x_scales, w_words, w_scales, wa, wb_
                 nc.sync.dma_start(out=tile[:], in_=rows[:, :, a * width:(a + 1) * width])
                 wa_raw[(e, a)] = tile
 
-        parts = [2, 1, 1, 1]
+        parts = [2, 1, 1, 2]
+        vector_m = [0, 16, 32, 48]
+        w_raw = {}
+        wb_raw = {}
+
+        def load_words(name, words, experts, views, dtype):
+            count = len(experts)
+            rows = words[experts[0]:experts[0] + count]
+            width = rows.shape[2]
+            tile = sbuf("%s%d" % (name, experts[0]), [P, count * width], I32)
+            nc.sync.dma_start(out=tile[:].rearrange("p (e c) -> p e c", e=count), in_=rows.rearrange("e p c -> p e c"))
+            for i, e in enumerate(experts):
+                views[e] = tile[:, i * width:(i + 1) * width].bitcast(dtype)
+
+        w_rows = w_words[:, 0].bitcast(I32)
+        wb_rows = wb_words[:, 0].rearrange("e p n d -> e p (n d)").bitcast(I32)
+
         nc.sync.dma_start(offsets[:], offs)
         nc.sync.dma_start(out=x_w[:].bitcast(I32), in_=x_words[0].rearrange("p t d -> p (t d)").bitcast(I32))
         for q in range(4):
@@ -62,27 +78,14 @@ def tile_moe_elr_s_relu_kernel(tc, x_words, x_scales, w_words, w_scales, wa, wb_
                 in_=w_scales[:, 0, 4 * q:4 * q + 4, :].bitcast(I32).rearrange("e r c -> r e c"),
             )
         load_wa(2, parts[2])
-        load_wa(3, parts[3])
         for q in range(4):
             nc.sync.dma_start(out=wb_s_raw[32 * q:32 * q + 16, :].bitcast(I32), in_=wb_scales[:, 0, 4 * q:4 * q + 4, :].bitcast(I32))
-        w_raw = {}
-        wb_raw = {}
-
-        def load_packed():
-            packed = sbuf("packed", [P, E * (N // 2 + N)], I32, tag="wa_raw1_0")
-            nc.sync.dma_start(
-                out=packed[:, 0:E * N // 2].rearrange("p (e c) -> p e c", e=E),
-                in_=w_words[:, 0].bitcast(I32).rearrange("e p c -> p e c"),
-            )
-            for pair in range(E // 2):
-                first = E * N // 2 + pair * 2 * N
-                nc.sync.dma_start(
-                    out=packed[:, first:first + 2 * N].rearrange("p (e c) -> p e c", e=2),
-                    in_=wb_words[2 * pair:2 * pair + 2, 0].rearrange("e p n d -> p e (n d)").bitcast(I32),
-                )
-            for e in range(E):
-                w_raw[e] = packed[:, e * N // 2:(e + 1) * N // 2].bitcast(U16)
-                wb_raw[e] = packed[:, E * N // 2 + e * N:E * N // 2 + (e + 1) * N]
+        load_words("w_raw", w_rows, [0, 1], w_raw, U16)
+        load_words("wb_raw", wb_rows, [0], wb_raw, I32)
+        load_wa(3, parts[3])
+        load_words("wb_raw", wb_rows, [1], wb_raw, I32)
+        load_words("w_raw", w_rows, [2, 3], w_raw, U16)
+        load_words("wb_raw", wb_rows, [2, 3], wb_raw, I32)
 
         def deal(dst, src):
             nc.vector.tensor_copy(
@@ -108,7 +111,11 @@ def tile_moe_elr_s_relu_kernel(tc, x_words, x_scales, w_words, w_scales, wa, wb_
             per = P // parts[e]
             for a in range(parts[e]):
                 src = wa_raw[(e, a)][:].rearrange("p j (m t) -> p m j t", t=PACK)
-                nc.scalar.copy(out=dst[:, a * per:(a + 1) * per], in_=src)
+                cut = per - vector_m[e] if a == parts[e] - 1 else per
+                if cut > 0:
+                    nc.scalar.copy(out=dst[:, a * per:a * per + cut], in_=src[:, 0:cut])
+                if cut < per:
+                    nc.vector.tensor_copy(out=dst[:, a * per + cut:(a + 1) * per], in_=src[:, cut:per])
 
         wa_w = {}
         wa_s = {}
@@ -138,14 +145,12 @@ def tile_moe_elr_s_relu_kernel(tc, x_words, x_scales, w_words, w_scales, wa, wb_
         h_bf = {}
 
         def round_h(e):
-            h_bf[e] = sbuf("h_bf%d" % e, [P, PACK * C], BF16)
+            tag = "wa_raw%d_%d" % (e + 1, parts[e + 1] - 1) if e + 1 < E else None
+            h_bf[e] = sbuf("h_bf%d" % e, [P, PACK * C], BF16, tag=tag)
             for s in range(C // HALF):
                 woven = h_bf[e][:, wide[s]].rearrange("p (u t) -> p u t", t=PACK)
                 sums = h_acc[(e, s)][:].rearrange("p t u -> p u t")
-                if e == 2:
-                    nc.scalar.activation(out=woven, in_=sums, func=RELU)
-                else:
-                    nc.vector.tensor_scalar_max(out=woven, in0=sums, scalar1=0.0)
+                nc.scalar.activation(out=woven, in_=sums, func=RELU)
 
         h_w = {}
         h_s = {}
@@ -153,28 +158,29 @@ def tile_moe_elr_s_relu_kernel(tc, x_words, x_scales, w_words, w_scales, wa, wb_
         def quantize_h(e):
             h_w[e] = sbuf("h_w%d" % e, [P, C], U32)
             h_s[e] = sbuf("h_s%d" % e, [P, C], U8)
-            for s, slots in enumerate(halves):
-                nc.vector.quantize_mx(out=h_w[e][:, slots].bitcast(FP8X4), scales=h_s[e][:, slots], in_=h_bf[e][:, wide[s]])
+            if e < E - 1:
+                nc.vector.quantize_mx(out=h_w[e][:].bitcast(FP8X4), scales=h_s[e][:], in_=h_bf[e][:])
+            else:
+                for s, slots in enumerate(halves):
+                    nc.vector.quantize_mx(out=h_w[e][:, slots].bitcast(FP8X4), scales=h_s[e][:, slots], in_=h_bf[e][:, wide[s]])
 
         w_w = {}
         w_s = {}
         wb_w = {}
-        wb_s = {}
-
-        def deal_scales():
-            wb_s[0] = sbuf("wb_s", [P, N], U8, tag="wa_bf2")
-            deal(wb_s[0][:], wb_s_raw[:])
-            for e in range(E):
-                w_s[e] = sbuf("w_s%d" % e, [P, N], U8)
-                deal(w_s[e][:], w_s_raw[:, e * N:(e + 1) * N])
+        wb_s = sbuf("wb_s", [P, N], U8)
 
         def deal_weights(e):
             w_w[e] = sbuf("w_w%d" % e, [P, 2 * N], U8)
+            w_s[e] = sbuf("w_s%d" % e, [P, N], U8)
             wb_w[e] = sbuf("wb_w%d" % e, [P, N], I32)
+            if e == 0:
+                deal(wb_s[:], wb_s_raw[:])
+            deal(w_s[e][:], w_s_raw[:, e * N:(e + 1) * N])
             deal(w_w[e][:].bitcast(U16), w_raw[e])
             deal(wb_w[e][:], wb_raw[e])
 
         out_rows = out_0.rearrange("(p t) j -> p t j", t=PACK)
+        out_words = out_1[0].rearrange("p j d -> p (j d)").bitcast(I32)
         y_s = sbuf("y_s", [P, E * C], U8)
 
         def result(e):
@@ -194,57 +200,45 @@ def tile_moe_elr_s_relu_kernel(tc, x_words, x_scales, w_words, w_scales, wa, wb_
                     )
                     nc.tensor.matmul_mx(
                         out=acc[:, t, :],
-                        lhsT=wb_w[e][:, cols].bitcast(FP8X4), lhsT_scale=wb_s[0][4 * e:P, cols],
+                        lhsT=wb_w[e][:, cols].bitcast(FP8X4), lhsT_scale=wb_s[4 * e:P, cols],
                         rhs=h_w[e][:, slots].bitcast(FP8X4), rhs_scale=h_s[e][:, slots],
                         start=False, stop=True,
                     )
-                woven = y_bf[:, wide[s]].rearrange("p (u t) -> p u t", t=PACK)
+                nc.scalar.copy(out=y_f[:, :, slots], in_=acc[:])
+                nc.vector.tensor_copy(
+                    out=y_bf[:, wide[s]].rearrange("p (c i t) -> p c t i", i=4, t=PACK),
+                    in_=y_f[:, :, slots].rearrange("p t (c i) -> p c t i", i=4),
+                )
                 if last:
-                    nc.vector.tensor_copy(out=woven, in_=acc[:].rearrange("p t u -> p u t"))
-                    nc.scalar.copy(out=y_f[:, :, slots], in_=acc[:])
-                    nc.sync.dma_start(out=out_rows[:, :, e * C + s * HALF:e * C + (s + 1) * HALF], in_=y_f[:, :, slots])
-                    nc.vector.quantize_mx(
-                        out=y_w[:, slots].bitcast(FP8X4),
-                        scales=y_s[:, e * C + s * HALF:e * C + (s + 1) * HALF],
-                        in_=y_bf[:, wide[s]],
-                    )
-                elif s == 0 or e < 2:
-                    nc.scalar.copy(out=y_f[:, :, slots], in_=acc[:])
-                    nc.scalar.copy(out=woven, in_=acc[:].rearrange("p t u -> p u t"))
-                else:
-                    nc.scalar.copy(out=y_f[:, :, slots], in_=acc[:])
-                    nc.vector.tensor_copy(
-                        out=y_bf[:, wide[s]].rearrange("p (c i t) -> p c t i", i=4, t=PACK),
-                        in_=y_f[:, :, slots].rearrange("p t (c i) -> p c t i", i=4),
-                    )
+                    cols = slice(e * C + s * HALF, e * C + (s + 1) * HALF)
+                    nc.sync.dma_start(out=out_rows[:, :, cols], in_=y_f[:, :, slots])
+                    nc.vector.quantize_mx(out=y_w[:, slots].bitcast(FP8X4), scales=y_s[:, cols], in_=y_bf[:, wide[s]])
+                    nc.sync.dma_start(out=out_words[:, cols], in_=y_w[:, slots].bitcast(I32))
             if not last:
-                nc.sync.dma_start(out=out_rows[:, :, e * C:(e + 1) * C], in_=y_f[:])
-                nc.vector.quantize_mx(out=y_w[:].bitcast(FP8X4), scales=y_s[:, e * C:(e + 1) * C], in_=y_bf[:])
-            nc.sync.dma_start(
-                out=out_1[0, :, e * C:(e + 1) * C, :].rearrange("p j d -> p (j d)").bitcast(I32),
-                in_=y_w[:].bitcast(I32),
-            )
+                cols = slice(e * C, (e + 1) * C)
+                nc.sync.dma_start(out=out_rows[:, :, cols], in_=y_f[:])
+                nc.vector.quantize_mx(out=y_w[:].bitcast(FP8X4), scales=y_s[:, cols], in_=y_bf[:])
+                nc.sync.dma_start(out=out_words[:, cols], in_=y_w[:].bitcast(I32))
+
+        def adapter_hidden(e):
+            round_h(e)
+            quantize_h(e)
+
+        def expert_result(e):
+            deal_weights(e)
+            result(e)
 
         for e in range(E):
             gather(e)
-        for e in range(E):
-            round_wa(e)
-            if e == 1:
-                load_packed()
-            quantize_wa(e)
-            hidden(e)
-            if e >= 1:
-                round_h(e - 1)
-                quantize_h(e - 1)
-        deal_scales()
-        deal_weights(0)
-        round_h(E - 1)
-        for e in range(E):
-            if e + 1 < E:
-                deal_weights(e + 1)
-            if e == 0:
-                quantize_h(E - 1)
-            result(e)
+        for step in range(E + 3):
+            if step < E:
+                round_wa(step)
+                quantize_wa(step)
+                hidden(step)
+            if 0 <= step - 1 < E:
+                adapter_hidden(step - 1)
+            if 0 <= step - 3 < E:
+                expert_result(step - 3)
 
         for q in range(4):
             queue = nc.sync if q % 2 == 0 else nc.scalar

@@ -49,43 +49,35 @@ def tile_moe_elr_s_relu_kernel(tc, x_words, x_scales, w_words, w_scales, wa, wb_
                 nc.sync.dma_start(out=tile[:], in_=rows[:, :, a * width:(a + 1) * width])
                 wa_raw[(e, a)] = tile
 
-        parts = [2, 1, 1, 2]
-        vector_m = [0, 16, 32, 48]
+        parts = [2, 2, 1, 1]
+        vector_m = [0, 0, 16, 64]
         w_raw = {}
         wb_raw = {}
 
-        def load_words(name, words, experts, views, dtype):
-            count = len(experts)
-            rows = words[experts[0]:experts[0] + count]
-            width = rows.shape[2]
-            tile = sbuf("%s%d" % (name, experts[0]), [P, count * width], I32)
-            nc.sync.dma_start(out=tile[:].rearrange("p (e c) -> p e c", e=count), in_=rows.rearrange("e p c -> p e c"))
-            for i, e in enumerate(experts):
-                views[e] = tile[:, i * width:(i + 1) * width].bitcast(dtype)
-
-        w_rows = w_words[:, 0].bitcast(I32)
-        wb_rows = wb_words[:, 0].rearrange("e p n d -> e p (n d)").bitcast(I32)
+        def load_packed(e):
+            w_raw[e] = sbuf("w_raw%d" % e, [P, N // 2], I32)
+            nc.sync.dma_start(out=w_raw[e][:], in_=w_words[e, 0].bitcast(I32))
+            wb_raw[e] = sbuf("wb_raw%d" % e, [P, N], I32)
+            nc.sync.dma_start(out=wb_raw[e][:], in_=wb_words[e, 0].rearrange("p n d -> p (n d)").bitcast(I32))
 
         nc.sync.dma_start(offsets[:], offs)
         nc.sync.dma_start(out=x_w[:].bitcast(I32), in_=x_words[0].rearrange("p t d -> p (t d)").bitcast(I32))
         for q in range(4):
-            nc.scalar.dma_start(out=x_s[32 * q:32 * q + 4, :].bitcast(I32), in_=x_scales[0, 4 * q:4 * q + 4, :].bitcast(I32))
+            nc.sync.dma_start(out=x_s[32 * q:32 * q + 4, :].bitcast(I32), in_=x_scales[0, 4 * q:4 * q + 4, :].bitcast(I32))
         load_wa(0, parts[0])
-        load_wa(1, parts[1])
         for q in range(4):
             nc.sync.dma_start(
                 out=w_s_raw[32 * q:32 * q + 4, :].bitcast(I32).rearrange("r (e c) -> r e c", e=E),
                 in_=w_scales[:, 0, 4 * q:4 * q + 4, :].bitcast(I32).rearrange("e r c -> r e c"),
             )
-        load_wa(2, parts[2])
+        load_wa(1, parts[1])
         for q in range(4):
             nc.sync.dma_start(out=wb_s_raw[32 * q:32 * q + 16, :].bitcast(I32), in_=wb_scales[:, 0, 4 * q:4 * q + 4, :].bitcast(I32))
-        load_words("w_raw", w_rows, [0, 1], w_raw, U16)
-        load_words("wb_raw", wb_rows, [0], wb_raw, I32)
+        load_wa(2, parts[2])
+        load_packed(0)
         load_wa(3, parts[3])
-        load_words("wb_raw", wb_rows, [1], wb_raw, I32)
-        load_words("w_raw", w_rows, [2, 3], w_raw, U16)
-        load_words("wb_raw", wb_rows, [2, 3], wb_raw, I32)
+        for e in range(1, E):
+            load_packed(e)
 
         def deal(dst, src):
             nc.vector.tensor_copy(
@@ -176,8 +168,8 @@ def tile_moe_elr_s_relu_kernel(tc, x_words, x_scales, w_words, w_scales, wa, wb_
             if e == 0:
                 deal(wb_s[:], wb_s_raw[:])
             deal(w_s[e][:], w_s_raw[:, e * N:(e + 1) * N])
-            deal(w_w[e][:].bitcast(U16), w_raw[e])
-            deal(wb_w[e][:], wb_raw[e])
+            deal(w_w[e][:].bitcast(U16), w_raw[e][:].bitcast(U16))
+            deal(wb_w[e][:], wb_raw[e][:])
 
         out_rows = out_0.rearrange("(p t) j -> p t j", t=PACK)
         out_words = out_1[0].rearrange("p j d -> p (j d)").bitcast(I32)
@@ -211,14 +203,12 @@ def tile_moe_elr_s_relu_kernel(tc, x_words, x_scales, w_words, w_scales, wa, wb_
                 )
                 if last:
                     cols = slice(e * C + s * HALF, e * C + (s + 1) * HALF)
-                    nc.sync.dma_start(out=out_rows[:, :, cols], in_=y_f[:, :, slots])
                     nc.vector.quantize_mx(out=y_w[:, slots].bitcast(FP8X4), scales=y_s[:, cols], in_=y_bf[:, wide[s]])
-                    nc.sync.dma_start(out=out_words[:, cols], in_=y_w[:, slots].bitcast(I32))
+            cols = slice(e * C, (e + 1) * C)
+            nc.sync.dma_start(out=out_rows[:, :, cols], in_=y_f[:])
             if not last:
-                cols = slice(e * C, (e + 1) * C)
-                nc.sync.dma_start(out=out_rows[:, :, cols], in_=y_f[:])
                 nc.vector.quantize_mx(out=y_w[:].bitcast(FP8X4), scales=y_s[:, cols], in_=y_bf[:])
-                nc.sync.dma_start(out=out_words[:, cols], in_=y_w[:].bitcast(I32))
+            nc.sync.dma_start(out=out_words[:, cols], in_=y_w[:].bitcast(I32))
 
         def adapter_hidden(e):
             round_h(e)

@@ -18,6 +18,7 @@ RELU = mybir.ActivationFunctionType.Relu
 P = 128
 PACK = 4
 HALF = 128
+WINDOW = 1536
 
 
 def tile_moe_elr_s_relu_kernel(tc, x_words, x_scales, w_words, w_scales, wa, wb_words, wb_scales, offs, out_0, out_1, out_2):
@@ -31,13 +32,15 @@ def tile_moe_elr_s_relu_kernel(tc, x_words, x_scales, w_words, w_scales, wa, wb_
             return keep.tile(shape, dtype, name=name, tag=tag or name, align_bytes=64)
 
         offsets = keep.tile([P, E * C // 16], U16, name="offsets")
-        x_w = sbuf("x_w", [P, T], U32)
-        x_s = sbuf("x_s", [P, T], U8)
+        x_w = sbuf("x_w", [P, WINDOW], I32)
+        x_s = sbuf("x_s", [P, WINDOW], U8)
         w_s_raw = sbuf("w_s_raw", [P, E * N], U8)
         wb_s_raw = sbuf("wb_s_raw", [P, N], U8)
-        nc.vector.memset(x_s[:].bitcast(I32), 0)
+        nc.vector.memset(x_s[:, 0:T].bitcast(I32), 0)
         nc.vector.memset(w_s_raw[:].bitcast(I32), 0)
         nc.vector.memset(wb_s_raw[:].bitcast(I32), 0)
+        nc.vector.memset(x_w[:, T:WINDOW], 0)
+        nc.vector.memset(x_s[:, T:WINDOW].bitcast(I32), 0)
 
         wa_raw = {}
 
@@ -49,8 +52,8 @@ def tile_moe_elr_s_relu_kernel(tc, x_words, x_scales, w_words, w_scales, wa, wb_
                 nc.sync.dma_start(out=tile[:], in_=rows[:, :, a * width:(a + 1) * width])
                 wa_raw[(e, a)] = tile
 
-        parts = [2, 2, 1, 1]
-        vector_m = [0, 0, 16, 64]
+        parts = [2, 2, 1, 2]
+        vector_m = [0, 0, 48, 48]
         w_raw = {}
         wb_raw = {}
 
@@ -60,10 +63,10 @@ def tile_moe_elr_s_relu_kernel(tc, x_words, x_scales, w_words, w_scales, wa, wb_
             wb_raw[e] = sbuf("wb_raw%d" % e, [P, N], I32)
             nc.sync.dma_start(out=wb_raw[e][:], in_=wb_words[e, 0].rearrange("p n d -> p (n d)").bitcast(I32))
 
+        nc.sync.dma_start(out=x_w[:, 0:T], in_=x_words[0].rearrange("p t d -> p (t d)").bitcast(I32))
         nc.sync.dma_start(offsets[:], offs)
-        nc.sync.dma_start(out=x_w[:].bitcast(I32), in_=x_words[0].rearrange("p t d -> p (t d)").bitcast(I32))
         for q in range(4):
-            nc.sync.dma_start(out=x_s[32 * q:32 * q + 4, :].bitcast(I32), in_=x_scales[0, 4 * q:4 * q + 4, :].bitcast(I32))
+            nc.sync.dma_start(out=x_s[32 * q:32 * q + 4, 0:T].bitcast(I32), in_=x_scales[0, 4 * q:4 * q + 4, :].bitcast(I32))
         load_wa(0, parts[0])
         for q in range(4):
             nc.sync.dma_start(
@@ -79,21 +82,18 @@ def tile_moe_elr_s_relu_kernel(tc, x_words, x_scales, w_words, w_scales, wa, wb_
         for e in range(1, E):
             load_packed(e)
 
-        def deal(dst, src):
+        def deal(dst, src, order, count=1):
             nc.vector.tensor_copy(
-                out=dst.rearrange("p (t m) -> p m t", t=PACK),
-                in_=src.rearrange("p (m t) -> p m t", t=PACK),
+                out=dst.rearrange("p (e t m) -> p e " + order, e=count, t=PACK),
+                in_=src.rearrange("p (e m t) -> p e " + order, e=count, t=PACK),
             )
 
-        xg_w = {}
-        xg_s = {}
-
-        def gather(e):
-            part = offsets[:, e * C // 16:(e + 1) * C // 16]
-            xg_w[e] = sbuf("xg_w%d" % e, [P, C], U32)
-            xg_s[e] = sbuf("xg_s%d" % e, [P, C], U8)
-            nc.vector.tensor_copy(xg_w[e][:], x_w[:].indirect(part))
-            nc.vector.tensor_copy(xg_s[e][:], x_s[:].indirect(part))
+        xg_all_w = sbuf("xg_w", [P, E * C], U32)
+        xg_all_s = sbuf("xg_s", [P, E * C], U8)
+        nc.vector.tensor_copy(xg_all_w[:], x_w[:].bitcast(U32).indirect(offsets[:]))
+        nc.vector.tensor_copy(xg_all_s[:], x_s[:].indirect(offsets[:]))
+        xg_w = [xg_all_w[:, e * C:(e + 1) * C] for e in range(E)]
+        xg_s = [xg_all_s[:, e * C:(e + 1) * C] for e in range(E)]
 
         wa_bf = {}
 
@@ -142,7 +142,10 @@ def tile_moe_elr_s_relu_kernel(tc, x_words, x_scales, w_words, w_scales, wa, wb_
             for s in range(C // HALF):
                 woven = h_bf[e][:, wide[s]].rearrange("p (u t) -> p u t", t=PACK)
                 sums = h_acc[(e, s)][:].rearrange("p t u -> p u t")
-                nc.scalar.activation(out=woven, in_=sums, func=RELU)
+                if (e, s) == (0, 1):
+                    nc.vector.tensor_scalar_max(out=woven, in0=sums, scalar1=0.0)
+                else:
+                    nc.scalar.activation(out=woven, in_=sums, func=RELU)
 
         h_w = {}
         h_s = {}
@@ -157,19 +160,19 @@ def tile_moe_elr_s_relu_kernel(tc, x_words, x_scales, w_words, w_scales, wa, wb_
                     nc.vector.quantize_mx(out=h_w[e][:, slots].bitcast(FP8X4), scales=h_s[e][:, slots], in_=h_bf[e][:, wide[s]])
 
         w_w = {}
-        w_s = {}
         wb_w = {}
+        w_s = {}
         wb_s = sbuf("wb_s", [P, N], U8)
 
         def deal_weights(e):
             w_w[e] = sbuf("w_w%d" % e, [P, 2 * N], U8)
-            w_s[e] = sbuf("w_s%d" % e, [P, N], U8)
             wb_w[e] = sbuf("wb_w%d" % e, [P, N], I32)
             if e == 0:
-                deal(wb_s[:], wb_s_raw[:])
-            deal(w_s[e][:], w_s_raw[:, e * N:(e + 1) * N])
-            deal(w_w[e][:].bitcast(U16), w_raw[e][:].bitcast(U16))
-            deal(wb_w[e][:], wb_raw[e][:])
+                deal(wb_s[:], wb_s_raw[:], "m t")
+                w_s[0] = sbuf("w_s", [P, E * N], U8, tag="wa_bf0")
+                deal(w_s[0][:], w_s_raw[:], "m t", E)
+            deal(w_w[e][:].bitcast(U16), w_raw[e][:].bitcast(U16), "m t")
+            deal(wb_w[e][:], wb_raw[e][:], "m t")
 
         out_rows = out_0.rearrange("(p t) j -> p t j", t=PACK)
         out_words = out_1[0].rearrange("p j d -> p (j d)").bitcast(I32)
@@ -186,7 +189,7 @@ def tile_moe_elr_s_relu_kernel(tc, x_words, x_scales, w_words, w_scales, wa, wb_
                     cols = slice(t * P, (t + 1) * P)
                     nc.tensor.matmul_mx(
                         out=acc[:, t, :],
-                        lhsT=w_w[e][:, 2 * t * P:2 * (t + 1) * P].bitcast(FP4X4), lhsT_scale=w_s[e][:, cols],
+                        lhsT=w_w[e][:, 2 * t * P:2 * (t + 1) * P].bitcast(FP4X4), lhsT_scale=w_s[0][:, e * N + t * P:e * N + (t + 1) * P],
                         rhs=xg_w[e][:, slots].bitcast(FP8X4), rhs_scale=xg_s[e][:, slots],
                         start=True, stop=False,
                     )
@@ -218,8 +221,6 @@ def tile_moe_elr_s_relu_kernel(tc, x_words, x_scales, w_words, w_scales, wa, wb_
             deal_weights(e)
             result(e)
 
-        for e in range(E):
-            gather(e)
         for step in range(E + 3):
             if step < E:
                 round_wa(step)

@@ -17,16 +17,22 @@ RELU = mybir.ActivationFunctionType.Relu
 
 P = 128
 PACK = 4
-HALF = 128
+QUADRANTS = 4
+BANK_SLOTS = 128
+BANKS = 4
+LINE = 4
 WINDOW = 1536
+WA_PARTS = (2, 1, 1, 2)
+VECTOR_GROUPS = (0, 48, 48, 48)
+VECTOR_BANK = (0, 1)
 
 
 def tile_moe_elr_s_relu_kernel(tc, x_words, x_scales, w_words, w_scales, wa, wb_words, wb_scales, offs, out_0, out_1, out_2):
     nc = tc.nc
     with ExitStack() as ctx:
         keep = ctx.enter_context(tc.tile_pool(name="keep", bufs=1))
-        psum_h = ctx.enter_context(tc.psum_pool(name="psum_h", bufs=4))
-        psum_y = ctx.enter_context(tc.psum_pool(name="psum_y", bufs=4))
+        psum_h = ctx.enter_context(tc.psum_pool(name="psum_h", bufs=BANKS))
+        psum_y = ctx.enter_context(tc.psum_pool(name="psum_y", bufs=BANKS))
 
         def sbuf(name, shape, dtype, tag=None):
             return keep.tile(shape, dtype, name=name, tag=tag or name, align_bytes=64)
@@ -43,19 +49,15 @@ def tile_moe_elr_s_relu_kernel(tc, x_words, x_scales, w_words, w_scales, wa, wb_
         nc.vector.memset(x_s[:, T:WINDOW].bitcast(I32), 0)
 
         wa_raw = {}
-
-        def load_wa(e, parts):
-            width = H // parts
-            rows = wa[e].rearrange("(p j) c -> p j c", j=PACK)
-            for a in range(parts):
-                tile = sbuf("wa_raw%d_%d" % (e, a), [P, PACK, width], F32)
-                nc.sync.dma_start(out=tile[:], in_=rows[:, :, a * width:(a + 1) * width])
-                wa_raw[(e, a)] = tile
-
-        parts = [2, 2, 1, 2]
-        vector_m = [0, 0, 48, 48]
         w_raw = {}
         wb_raw = {}
+
+        def load_wa(e):
+            width = H // WA_PARTS[e]
+            rows = wa[e].rearrange("(p j) c -> p j c", j=PACK)
+            for a in range(WA_PARTS[e]):
+                wa_raw[(e, a)] = sbuf("wa_raw%d_%d" % (e, a), [P, PACK, width], F32)
+                nc.sync.dma_start(out=wa_raw[(e, a)][:], in_=rows[:, :, a * width:(a + 1) * width])
 
         def load_packed(e):
             w_raw[e] = sbuf("w_raw%d" % e, [P, N // 2], I32)
@@ -65,172 +67,148 @@ def tile_moe_elr_s_relu_kernel(tc, x_words, x_scales, w_words, w_scales, wa, wb_
 
         nc.sync.dma_start(out=x_w[:, 0:T], in_=x_words[0].rearrange("p t d -> p (t d)").bitcast(I32))
         nc.sync.dma_start(offsets[:], offs)
-        for q in range(4):
+        for q in range(QUADRANTS):
             nc.sync.dma_start(out=x_s[32 * q:32 * q + 4, 0:T].bitcast(I32), in_=x_scales[0, 4 * q:4 * q + 4, :].bitcast(I32))
-        load_wa(0, parts[0])
-        for q in range(4):
+        load_wa(0)
+        for q in range(QUADRANTS):
             nc.sync.dma_start(
                 out=w_s_raw[32 * q:32 * q + 4, :].bitcast(I32).rearrange("r (e c) -> r e c", e=E),
                 in_=w_scales[:, 0, 4 * q:4 * q + 4, :].bitcast(I32).rearrange("e r c -> r e c"),
             )
-        load_wa(1, parts[1])
-        for q in range(4):
-            nc.sync.dma_start(out=wb_s_raw[32 * q:32 * q + 16, :].bitcast(I32), in_=wb_scales[:, 0, 4 * q:4 * q + 4, :].bitcast(I32))
-        load_wa(2, parts[2])
+        load_wa(1)
+        for q in range(QUADRANTS):
+            nc.sync.dma_start(out=wb_s_raw[32 * q:32 * q + 4 * E, :].bitcast(I32), in_=wb_scales[:, 0, 4 * q:4 * q + 4, :].bitcast(I32))
+        load_wa(2)
         load_packed(0)
-        load_wa(3, parts[3])
+        load_wa(3)
         for e in range(1, E):
             load_packed(e)
 
-        def deal(dst, src, order, count=1):
+        slot_w = sbuf("slot_w", [P, E * C], U32)
+        slot_s = sbuf("slot_s", [P, E * C], U8)
+        nc.vector.tensor_copy(slot_w[:], x_w[:].bitcast(U32).indirect(offsets[:]))
+        nc.vector.tensor_copy(slot_s[:], x_s[:].indirect(offsets[:]))
+
+        banks = range(C // BANK_SLOTS)
+
+        def span(index, width):
+            return slice(index * width, (index + 1) * width)
+
+        def deal(dst, src, count=1):
             nc.vector.tensor_copy(
-                out=dst.rearrange("p (e t m) -> p e " + order, e=count, t=PACK),
-                in_=src.rearrange("p (e m t) -> p e " + order, e=count, t=PACK),
+                out=dst.rearrange("p (e t m) -> p e m t", e=count, t=PACK),
+                in_=src.rearrange("p (e m t) -> p e m t", e=count, t=PACK),
             )
 
-        xg_all_w = sbuf("xg_w", [P, E * C], U32)
-        xg_all_s = sbuf("xg_s", [P, E * C], U8)
-        nc.vector.tensor_copy(xg_all_w[:], x_w[:].bitcast(U32).indirect(offsets[:]))
-        nc.vector.tensor_copy(xg_all_s[:], x_s[:].indirect(offsets[:]))
-        xg_w = [xg_all_w[:, e * C:(e + 1) * C] for e in range(E)]
-        xg_s = [xg_all_s[:, e * C:(e + 1) * C] for e in range(E)]
-
-        wa_bf = {}
-
-        def round_wa(e):
-            wa_bf[e] = sbuf("wa_bf%d" % e, [P, PACK * H], BF16)
-            dst = wa_bf[e][:].rearrange("p (t m j) -> p m j t", t=PACK, j=PACK)
-            per = P // parts[e]
-            for a in range(parts[e]):
-                src = wa_raw[(e, a)][:].rearrange("p j (m t) -> p m j t", t=PACK)
-                cut = per - vector_m[e] if a == parts[e] - 1 else per
-                if cut > 0:
-                    nc.scalar.copy(out=dst[:, a * per:a * per + cut], in_=src[:, 0:cut])
-                if cut < per:
-                    nc.vector.tensor_copy(out=dst[:, a * per + cut:(a + 1) * per], in_=src[:, cut:per])
-
-        wa_w = {}
-        wa_s = {}
-
-        def quantize_wa(e):
-            wa_w[e] = sbuf("wa_w%d" % e, [P, H], U32)
-            wa_s[e] = sbuf("wa_s%d" % e, [P, H], U8)
-            nc.vector.quantize_mx(out=wa_w[e][:].bitcast(FP8X4), scales=wa_s[e][:], in_=wa_bf[e][:])
-
-        halves = [slice(s * HALF, (s + 1) * HALF) for s in range(C // HALF)]
-        wide = [slice(s * HALF * PACK, (s + 1) * HALF * PACK) for s in range(C // HALF)]
         h_acc = {}
 
-        def hidden(e):
-            for s, slots in enumerate(halves):
-                acc = psum_h.tile([P, PACK, HALF], F32, name="acc_h")
-                h_acc[(e, s)] = acc
+        def adapter_first(e):
+            wa_bf = sbuf("wa_bf%d" % e, [P, PACK * H], BF16)
+            dst = wa_bf[:].rearrange("p (t m j) -> p m j t", t=PACK, j=PACK)
+            groups = P // WA_PARTS[e]
+            for a in range(WA_PARTS[e]):
+                src = wa_raw[(e, a)][:].rearrange("p j (m t) -> p m j t", t=PACK)
+                cut = groups - VECTOR_GROUPS[e] if a == WA_PARTS[e] - 1 else groups
+                nc.scalar.copy(out=dst[:, a * groups:a * groups + cut], in_=src[:, 0:cut])
+                if cut < groups:
+                    nc.vector.tensor_copy(out=dst[:, a * groups + cut:(a + 1) * groups], in_=src[:, cut:groups])
+            wa_w = sbuf("wa_w%d" % e, [P, H], U32)
+            wa_s = sbuf("wa_s%d" % e, [P, H], U8)
+            nc.vector.quantize_mx(out=wa_w[:].bitcast(FP8X4), scales=wa_s[:], in_=wa_bf[:])
+            for b in banks:
+                slots = span(e * len(banks) + b, BANK_SLOTS)
+                h_acc[(e, b)] = psum_h.tile([P, PACK, BANK_SLOTS], F32, name="acc_h")
                 for t in range(PACK):
-                    cols = slice(t * P, (t + 1) * P)
                     nc.tensor.matmul_mx(
-                        out=acc[:, t, :],
-                        lhsT=wa_w[e][:, cols].bitcast(FP8X4), lhsT_scale=wa_s[e][:, cols],
-                        rhs=xg_w[e][:, slots].bitcast(FP8X4), rhs_scale=xg_s[e][:, slots],
+                        out=h_acc[(e, b)][:, t, :],
+                        lhsT=wa_w[:, span(t, P)].bitcast(FP8X4), lhsT_scale=wa_s[:, span(t, P)],
+                        rhs=slot_w[:, slots].bitcast(FP8X4), rhs_scale=slot_s[:, slots],
                         start=True, stop=True,
                     )
-
-        h_bf = {}
-
-        def round_h(e):
-            tag = "wa_raw%d_%d" % (e + 1, parts[e + 1] - 1) if e + 1 < E else None
-            h_bf[e] = sbuf("h_bf%d" % e, [P, PACK * C], BF16, tag=tag)
-            for s in range(C // HALF):
-                woven = h_bf[e][:, wide[s]].rearrange("p (u t) -> p u t", t=PACK)
-                sums = h_acc[(e, s)][:].rearrange("p t u -> p u t")
-                if (e, s) == (0, 1):
-                    nc.vector.tensor_scalar_max(out=woven, in0=sums, scalar1=0.0)
-                else:
-                    nc.scalar.activation(out=woven, in_=sums, func=RELU)
 
         h_w = {}
         h_s = {}
 
-        def quantize_h(e):
+        def adapter_hidden(e):
+            tag = "wa_raw%d_%d" % (e + 1, WA_PARTS[e + 1] - 1) if e + 1 < E else None
+            h_bf = sbuf("h_bf%d" % e, [P, PACK * C], BF16, tag=tag)
+            for b in banks:
+                woven = h_bf[:, span(b, PACK * BANK_SLOTS)].rearrange("p (u t) -> p u t", t=PACK)
+                sums = h_acc[(e, b)][:].rearrange("p t u -> p u t")
+                if (e, b) == VECTOR_BANK:
+                    nc.vector.tensor_scalar_max(out=woven, in0=sums, scalar1=0.0)
+                else:
+                    nc.scalar.activation(out=woven, in_=sums, func=RELU)
             h_w[e] = sbuf("h_w%d" % e, [P, C], U32)
             h_s[e] = sbuf("h_s%d" % e, [P, C], U8)
-            if e < E - 1:
-                nc.vector.quantize_mx(out=h_w[e][:].bitcast(FP8X4), scales=h_s[e][:], in_=h_bf[e][:])
-            else:
-                for s, slots in enumerate(halves):
-                    nc.vector.quantize_mx(out=h_w[e][:, slots].bitcast(FP8X4), scales=h_s[e][:, slots], in_=h_bf[e][:, wide[s]])
+            width = BANK_SLOTS if e == E - 1 else C
+            for piece in range(C // width):
+                nc.vector.quantize_mx(
+                    out=h_w[e][:, span(piece, width)].bitcast(FP8X4),
+                    scales=h_s[e][:, span(piece, width)],
+                    in_=h_bf[:, span(piece, PACK * width)],
+                )
 
-        w_w = {}
-        wb_w = {}
-        w_s = {}
-        wb_s = sbuf("wb_s", [P, N], U8)
+        dealt_s = {}
 
-        def deal_weights(e):
-            w_w[e] = sbuf("w_w%d" % e, [P, 2 * N], U8)
-            wb_w[e] = sbuf("wb_w%d" % e, [P, N], I32)
-            if e == 0:
-                deal(wb_s[:], wb_s_raw[:], "m t")
-                w_s[0] = sbuf("w_s", [P, E * N], U8, tag="wa_bf0")
-                deal(w_s[0][:], w_s_raw[:], "m t", E)
-            deal(w_w[e][:].bitcast(U16), w_raw[e][:].bitcast(U16), "m t")
-            deal(wb_w[e][:], wb_raw[e][:], "m t")
+        def deal_scales():
+            dealt_s["wb"] = sbuf("wb_s", [P, N], U8)
+            deal(dealt_s["wb"][:], wb_s_raw[:])
+            dealt_s["w"] = sbuf("w_s", [P, E * N], U8, tag="wa_bf0")
+            deal(dealt_s["w"][:], w_s_raw[:], E)
 
         out_rows = out_0.rearrange("(p t) j -> p t j", t=PACK)
         out_words = out_1[0].rearrange("p j d -> p (j d)").bitcast(I32)
         y_s = sbuf("y_s", [P, E * C], U8)
 
-        def result(e):
-            last = e == E - 1
+        def expert_result(e):
+            w_w = sbuf("w_w%d" % e, [P, 2 * N], U8)
+            wb_w = sbuf("wb_w%d" % e, [P, N], I32)
+            deal(w_w[:].bitcast(U16), w_raw[e][:].bitcast(U16))
+            deal(wb_w[:], wb_raw[e][:])
             y_f = sbuf("y_f%d" % e, [P, PACK, C], F32)
             y_bf = sbuf("y_bf%d" % e, [P, PACK * C], BF16)
             y_w = sbuf("y_w%d" % e, [P, C], U32)
-            for s, slots in enumerate(halves):
-                acc = psum_y.tile([P, PACK, HALF], F32, name="acc_y")
+            last = e == E - 1
+            for b in banks:
+                own = span(b, BANK_SLOTS)
+                slots = span(e * len(banks) + b, BANK_SLOTS)
+                acc = psum_y.tile([P, PACK, BANK_SLOTS], F32, name="acc_y")
                 for t in range(PACK):
-                    cols = slice(t * P, (t + 1) * P)
                     nc.tensor.matmul_mx(
                         out=acc[:, t, :],
-                        lhsT=w_w[e][:, 2 * t * P:2 * (t + 1) * P].bitcast(FP4X4), lhsT_scale=w_s[0][:, e * N + t * P:e * N + (t + 1) * P],
-                        rhs=xg_w[e][:, slots].bitcast(FP8X4), rhs_scale=xg_s[e][:, slots],
+                        lhsT=w_w[:, span(t, 2 * P)].bitcast(FP4X4), lhsT_scale=dealt_s["w"][:, span(e * PACK + t, P)],
+                        rhs=slot_w[:, slots].bitcast(FP8X4), rhs_scale=slot_s[:, slots],
                         start=True, stop=False,
                     )
                     nc.tensor.matmul_mx(
                         out=acc[:, t, :],
-                        lhsT=wb_w[e][:, cols].bitcast(FP8X4), lhsT_scale=wb_s[4 * e:P, cols],
-                        rhs=h_w[e][:, slots].bitcast(FP8X4), rhs_scale=h_s[e][:, slots],
+                        lhsT=wb_w[:, span(t, P)].bitcast(FP8X4), lhsT_scale=dealt_s["wb"][4 * e:P, span(t, P)],
+                        rhs=h_w[e][:, own].bitcast(FP8X4), rhs_scale=h_s[e][:, own],
                         start=False, stop=True,
                     )
-                nc.scalar.copy(out=y_f[:, :, slots], in_=acc[:])
+                nc.scalar.copy(out=y_f[:, :, own], in_=acc[:])
                 nc.vector.tensor_copy(
-                    out=y_bf[:, wide[s]].rearrange("p (c i t) -> p c t i", i=4, t=PACK),
-                    in_=y_f[:, :, slots].rearrange("p t (c i) -> p c t i", i=4),
+                    out=y_bf[:, span(b, PACK * BANK_SLOTS)].rearrange("p (c i t) -> p c t i", i=LINE, t=PACK),
+                    in_=y_f[:, :, own].rearrange("p t (c i) -> p c t i", i=LINE),
                 )
                 if last:
-                    cols = slice(e * C + s * HALF, e * C + (s + 1) * HALF)
-                    nc.vector.quantize_mx(out=y_w[:, slots].bitcast(FP8X4), scales=y_s[:, cols], in_=y_bf[:, wide[s]])
-            cols = slice(e * C, (e + 1) * C)
-            nc.sync.dma_start(out=out_rows[:, :, cols], in_=y_f[:])
+                    nc.vector.quantize_mx(out=y_w[:, own].bitcast(FP8X4), scales=y_s[:, slots], in_=y_bf[:, span(b, PACK * BANK_SLOTS)])
+            nc.sync.dma_start(out=out_rows[:, :, span(e, C)], in_=y_f[:])
             if not last:
-                nc.vector.quantize_mx(out=y_w[:].bitcast(FP8X4), scales=y_s[:, cols], in_=y_bf[:])
-            nc.sync.dma_start(out=out_words[:, cols], in_=y_w[:].bitcast(I32))
-
-        def adapter_hidden(e):
-            round_h(e)
-            quantize_h(e)
-
-        def expert_result(e):
-            deal_weights(e)
-            result(e)
+                nc.vector.quantize_mx(out=y_w[:].bitcast(FP8X4), scales=y_s[:, span(e, C)], in_=y_bf[:])
+            nc.sync.dma_start(out=out_words[:, span(e, C)], in_=y_w[:].bitcast(I32))
 
         for step in range(E + 3):
             if step < E:
-                round_wa(step)
-                quantize_wa(step)
-                hidden(step)
+                adapter_first(step)
             if 0 <= step - 1 < E:
                 adapter_hidden(step - 1)
+            if step - 3 == 0:
+                deal_scales()
             if 0 <= step - 3 < E:
                 expert_result(step - 3)
 
-        for q in range(4):
+        for q in range(QUADRANTS):
             queue = nc.sync if q % 2 == 0 else nc.scalar
             queue.dma_start(out=out_2[0, 4 * q:4 * q + 4, :].bitcast(I32), in_=y_s[32 * q:32 * q + 4, :].bitcast(I32))

@@ -15,6 +15,8 @@ FP8X4 = mybir.dt.float8_e4m3fn_x4
 FP4X4 = mybir.dt.float4_e2m1fn_x4
 RELU = mybir.ActivationFunctionType.Relu
 
+ITEM_BYTES = {F32: 4, BF16: 2, I32: 4, U32: 4, U8: 1}
+
 P = 128
 PACK = 4
 QUADRANTS = 4
@@ -22,29 +24,39 @@ BANK_SLOTS = 128
 BANKS = 4
 LINE = 4
 WINDOW = 1536
-WA_PARTS = (2, 1, 1, 2)
-VECTOR_GROUPS = (0, 48, 48, 48)
-VECTOR_BANK = (0, 1)
+WA_PARTS = (2, 1, 1, 1)
+VECTOR_GROUPS = (0, 64, 96, 48)
 
 
 def tile_moe_elr_s_relu_kernel(tc, x_words, x_scales, w_words, w_scales, wa, wb_words, wb_scales, offs, out_0, out_1, out_2):
     nc = tc.nc
     with ExitStack() as ctx:
         keep = ctx.enter_context(tc.tile_pool(name="keep", bufs=1))
+        work = ctx.enter_context(tc.tile_pool(name="work", bufs=1))
         psum_h = ctx.enter_context(tc.psum_pool(name="psum_h", bufs=BANKS))
         psum_y = ctx.enter_context(tc.psum_pool(name="psum_y", bufs=BANKS))
 
-        def sbuf(name, shape, dtype, tag=None):
-            return keep.tile(shape, dtype, name=name, tag=tag or name, align_bytes=64)
+        start = {}
+        used = [0]
+
+        def sbuf(name, shape, dtype, over=None, skip=0):
+            if over is None:
+                start[name] = sum(used)
+                size = ITEM_BYTES[dtype]
+                for extent in shape[1:]:
+                    size = size * extent
+                used.append(size)
+            else:
+                start[name] = start[over] + skip
+            return work.tile(shape, dtype, name=name, tag=name, align_bytes=64, offset=start[name])
 
         offsets = keep.tile([P, E * C // 16], U16, name="offsets")
         x_w = sbuf("x_w", [P, WINDOW], I32)
         x_s = sbuf("x_s", [P, WINDOW], U8)
-        w_s_raw = sbuf("w_s_raw", [P, E * N], U8)
-        wb_s_raw = sbuf("wb_s_raw", [P, N], U8)
+        s_raw = sbuf("s_raw", [P, N], U8)
+        w_s = sbuf("w_s", [P, E * N], U8)
         nc.vector.memset(x_s[:, 0:T].bitcast(I32), 0)
-        nc.vector.memset(w_s_raw[:].bitcast(I32), 0)
-        nc.vector.memset(wb_s_raw[:].bitcast(I32), 0)
+        nc.vector.memset(w_s[:].bitcast(I32), 0)
         nc.vector.memset(x_w[:, T:WINDOW], 0)
         nc.vector.memset(x_s[:, T:WINDOW].bitcast(I32), 0)
 
@@ -65,6 +77,24 @@ def tile_moe_elr_s_relu_kernel(tc, x_words, x_scales, w_words, w_scales, wa, wb_
             wb_raw[e] = sbuf("wb_raw%d" % e, [P, N], I32)
             nc.sync.dma_start(out=wb_raw[e][:], in_=wb_words[e, 0].rearrange("p n d -> p (n d)").bitcast(I32))
 
+        def deal(dst, src, count=1):
+            nc.vector.tensor_copy(
+                out=dst.rearrange("p (e t m) -> p e m t", e=count, t=PACK),
+                in_=src.rearrange("p (e m t) -> p e m t", e=count, t=PACK),
+            )
+
+        dealt_s = {}
+
+        def deal_scales():
+            dealt_s["wb"] = sbuf("s_dealt", [P, N], U8)
+            deal(dealt_s["wb"][:], s_raw[:])
+            dealt_s["w"] = w_s
+            for q in range(QUADRANTS):
+                nc.sync.dma_start(
+                    out=w_s[32 * q:32 * q + 4, :].bitcast(I32).rearrange("r (e c) -> r e c", e=E),
+                    in_=dealt_s["wb"][32 * q + 16:32 * q + 32, :].bitcast(I32),
+                )
+
         nc.sync.dma_start(out=x_w[:, 0:T], in_=x_words[0].rearrange("p t d -> p (t d)").bitcast(I32))
         nc.sync.dma_start(offsets[:], offs)
         for q in range(QUADRANTS):
@@ -72,16 +102,16 @@ def tile_moe_elr_s_relu_kernel(tc, x_words, x_scales, w_words, w_scales, wa, wb_
         load_wa(0)
         for q in range(QUADRANTS):
             nc.sync.dma_start(
-                out=w_s_raw[32 * q:32 * q + 4, :].bitcast(I32).rearrange("r (e c) -> r e c", e=E),
+                out=s_raw[32 * q + 16:32 * q + 32, :].bitcast(I32),
                 in_=w_scales[:, 0, 4 * q:4 * q + 4, :].bitcast(I32).rearrange("e r c -> r e c"),
             )
         load_wa(1)
         for q in range(QUADRANTS):
-            nc.sync.dma_start(out=wb_s_raw[32 * q:32 * q + 4 * E, :].bitcast(I32), in_=wb_scales[:, 0, 4 * q:4 * q + 4, :].bitcast(I32))
+            nc.sync.dma_start(out=s_raw[32 * q:32 * q + 4 * E, :].bitcast(I32), in_=wb_scales[:, 0, 4 * q:4 * q + 4, :].bitcast(I32))
         load_wa(2)
-        load_packed(0)
         load_wa(3)
-        for e in range(1, E):
+        deal_scales()
+        for e in range(E):
             load_packed(e)
 
         slot_w = sbuf("slot_w", [P, E * C], U32)
@@ -94,17 +124,12 @@ def tile_moe_elr_s_relu_kernel(tc, x_words, x_scales, w_words, w_scales, wa, wb_
         def span(index, width):
             return slice(index * width, (index + 1) * width)
 
-        def deal(dst, src, count=1):
-            nc.vector.tensor_copy(
-                out=dst.rearrange("p (e t m) -> p e m t", e=count, t=PACK),
-                in_=src.rearrange("p (e m t) -> p e m t", e=count, t=PACK),
-            )
-
+        wa_bf = {}
         h_acc = {}
 
-        def adapter_first(e):
-            wa_bf = sbuf("wa_bf%d" % e, [P, PACK * H], BF16)
-            dst = wa_bf[:].rearrange("p (t m j) -> p m j t", t=PACK, j=PACK)
+        def round_wa(e):
+            wa_bf[e] = sbuf("wa_bf%d" % e, [P, PACK * H], BF16)
+            dst = wa_bf[e][:].rearrange("p (t m j) -> p m j t", t=PACK, j=PACK)
             groups = P // WA_PARTS[e]
             for a in range(WA_PARTS[e]):
                 src = wa_raw[(e, a)][:].rearrange("p j (m t) -> p m j t", t=PACK)
@@ -112,9 +137,11 @@ def tile_moe_elr_s_relu_kernel(tc, x_words, x_scales, w_words, w_scales, wa, wb_
                 nc.scalar.copy(out=dst[:, a * groups:a * groups + cut], in_=src[:, 0:cut])
                 if cut < groups:
                     nc.vector.tensor_copy(out=dst[:, a * groups + cut:(a + 1) * groups], in_=src[:, cut:groups])
-            wa_w = sbuf("wa_w%d" % e, [P, H], U32)
+
+        def first_product(e):
+            wa_w = sbuf("wa_w%d" % e, [P, H], U32, over="wb_raw0" if e == E - 1 else None)
             wa_s = sbuf("wa_s%d" % e, [P, H], U8)
-            nc.vector.quantize_mx(out=wa_w[:].bitcast(FP8X4), scales=wa_s[:], in_=wa_bf[:])
+            nc.vector.quantize_mx(out=wa_w[:].bitcast(FP8X4), scales=wa_s[:], in_=wa_bf[e][:])
             for b in banks:
                 slots = span(e * len(banks) + b, BANK_SLOTS)
                 h_acc[(e, b)] = psum_h.tile([P, PACK, BANK_SLOTS], F32, name="acc_h")
@@ -126,88 +153,130 @@ def tile_moe_elr_s_relu_kernel(tc, x_words, x_scales, w_words, w_scales, wa, wb_
                         start=True, stop=True,
                     )
 
+        h_bf = {}
         h_w = {}
         h_s = {}
 
-        def adapter_hidden(e):
-            tag = "wa_raw%d_%d" % (e + 1, WA_PARTS[e + 1] - 1) if e + 1 < E else None
-            h_bf = sbuf("h_bf%d" % e, [P, PACK * C], BF16, tag=tag)
+        def empty_h(e):
+            h_bf[e] = sbuf("h_bf%d" % e, [P, PACK * C], BF16, over="wa_raw%d_0" % (e + 1) if e + 1 < E else None)
             for b in banks:
-                woven = h_bf[:, span(b, PACK * BANK_SLOTS)].rearrange("p (u t) -> p u t", t=PACK)
-                sums = h_acc[(e, b)][:].rearrange("p t u -> p u t")
-                if (e, b) == VECTOR_BANK:
-                    nc.vector.tensor_scalar_max(out=woven, in0=sums, scalar1=0.0)
-                else:
-                    nc.scalar.activation(out=woven, in_=sums, func=RELU)
-            h_w[e] = sbuf("h_w%d" % e, [P, C], U32)
+                nc.scalar.activation(
+                    out=h_bf[e][:, span(b, PACK * BANK_SLOTS)].rearrange("p (u t) -> p u t", t=PACK),
+                    in_=h_acc[(e, b)][:].rearrange("p t u -> p u t"),
+                    func=RELU,
+                )
+
+        def quantise_h(e, over, skip=0):
+            h_w[e] = sbuf("h_w%d" % e, [P, C], U32, over=over, skip=skip)
             h_s[e] = sbuf("h_s%d" % e, [P, C], U8)
             width = BANK_SLOTS if e == E - 1 else C
             for piece in range(C // width):
                 nc.vector.quantize_mx(
                     out=h_w[e][:, span(piece, width)].bitcast(FP8X4),
                     scales=h_s[e][:, span(piece, width)],
-                    in_=h_bf[:, span(piece, PACK * width)],
+                    in_=h_bf[e][:, span(piece, PACK * width)],
                 )
-
-        dealt_s = {}
-
-        def deal_scales():
-            dealt_s["wb"] = sbuf("wb_s", [P, N], U8)
-            deal(dealt_s["wb"][:], wb_s_raw[:])
-            dealt_s["w"] = sbuf("w_s", [P, E * N], U8, tag="wa_bf0")
-            deal(dealt_s["w"][:], w_s_raw[:], E)
 
         out_rows = out_0.rearrange("(p t) j -> p t j", t=PACK)
         out_words = out_1[0].rearrange("p j d -> p (j d)").bitcast(I32)
         y_s = sbuf("y_s", [P, E * C], U8)
+        w_w = {}
+        wb_w = {}
+        y_acc = {}
+        y_f = {}
+        y_bf = {}
 
-        def expert_result(e):
-            w_w = sbuf("w_w%d" % e, [P, 2 * N], U8)
-            wb_w = sbuf("wb_w%d" % e, [P, N], I32)
-            deal(w_w[:].bitcast(U16), w_raw[e][:].bitcast(U16))
-            deal(wb_w[:], wb_raw[e][:])
-            y_f = sbuf("y_f%d" % e, [P, PACK, C], F32)
-            y_bf = sbuf("y_bf%d" % e, [P, PACK * C], BF16)
-            y_w = sbuf("y_w%d" % e, [P, C], U32)
-            last = e == E - 1
+        def deal_packed(e):
+            w_w[e] = sbuf("w_w%d" % e, [P, 2 * N], U8)
+            wb_w[e] = sbuf("wb_w%d" % e, [P, N], I32)
+            deal(w_w[e][:].bitcast(U16), w_raw[e][:].bitcast(U16))
+            deal(wb_w[e][:], wb_raw[e][:])
+
+        def second_product(e):
             for b in banks:
                 own = span(b, BANK_SLOTS)
                 slots = span(e * len(banks) + b, BANK_SLOTS)
                 acc = psum_y.tile([P, PACK, BANK_SLOTS], F32, name="acc_y")
+                y_acc[(e, b)] = acc
                 for t in range(PACK):
                     nc.tensor.matmul_mx(
                         out=acc[:, t, :],
-                        lhsT=w_w[:, span(t, 2 * P)].bitcast(FP4X4), lhsT_scale=dealt_s["w"][:, span(e * PACK + t, P)],
+                        lhsT=w_w[e][:, span(t, 2 * P)].bitcast(FP4X4), lhsT_scale=dealt_s["w"][:, span(e * PACK + t, P)],
                         rhs=slot_w[:, slots].bitcast(FP8X4), rhs_scale=slot_s[:, slots],
                         start=True, stop=False,
                     )
                     nc.tensor.matmul_mx(
                         out=acc[:, t, :],
-                        lhsT=wb_w[:, span(t, P)].bitcast(FP8X4), lhsT_scale=dealt_s["wb"][4 * e:P, span(t, P)],
+                        lhsT=wb_w[e][:, span(t, P)].bitcast(FP8X4), lhsT_scale=dealt_s["wb"][4 * e:P, span(t, P)],
                         rhs=h_w[e][:, own].bitcast(FP8X4), rhs_scale=h_s[e][:, own],
                         start=False, stop=True,
                     )
-                nc.scalar.copy(out=y_f[:, :, own], in_=acc[:])
-                nc.vector.tensor_copy(
-                    out=y_bf[:, span(b, PACK * BANK_SLOTS)].rearrange("p (c i t) -> p c t i", i=LINE, t=PACK),
-                    in_=y_f[:, :, own].rearrange("p t (c i) -> p c t i", i=LINE),
+
+        def empty_y(e):
+            y_f[e] = sbuf("y_f%d" % e, [P, PACK, C], F32)
+            for b in banks:
+                nc.scalar.copy(out=y_f[e][:, :, span(b, BANK_SLOTS)], in_=y_acc[(e, b)][:])
+            nc.sync.dma_start(out=out_rows[:, :, span(e, C)], in_=y_f[e][:])
+
+        def round_y(e, b):
+            if b == 0:
+                y_bf[e] = sbuf("y_bf%d" % e, [P, PACK * C], BF16)
+            nc.vector.tensor_copy(
+                out=y_bf[e][:, span(b, PACK * BANK_SLOTS)].rearrange("p (c i t) -> p c t i", i=LINE, t=PACK),
+                in_=y_f[e][:, :, span(b, BANK_SLOTS)].rearrange("p t (c i) -> p c t i", i=LINE),
+            )
+
+        def quantise_y(e):
+            y_w = sbuf("y_w%d" % e, [P, C], U32)
+            width = BANK_SLOTS if e == E - 1 else C
+            for piece in range(C // width):
+                nc.vector.quantize_mx(
+                    out=y_w[:, span(piece, width)].bitcast(FP8X4),
+                    scales=y_s[:, e * C + piece * width:e * C + (piece + 1) * width],
+                    in_=y_bf[e][:, span(piece, PACK * width)],
                 )
-                if last:
-                    nc.vector.quantize_mx(out=y_w[:, own].bitcast(FP8X4), scales=y_s[:, slots], in_=y_bf[:, span(b, PACK * BANK_SLOTS)])
-            nc.sync.dma_start(out=out_rows[:, :, span(e, C)], in_=y_f[:])
-            if not last:
-                nc.vector.quantize_mx(out=y_w[:].bitcast(FP8X4), scales=y_s[:, span(e, C)], in_=y_bf[:])
             nc.sync.dma_start(out=out_words[:, span(e, C)], in_=y_w[:].bitcast(I32))
 
-        for step in range(E + 3):
-            if step < E:
-                adapter_first(step)
-            if 0 <= step - 1 < E:
-                adapter_hidden(step - 1)
-            if step - 3 == 0:
-                deal_scales()
-            if 0 <= step - 3 < E:
-                expert_result(step - 3)
+        def round_y_all(e):
+            for b in banks:
+                round_y(e, b)
+
+        round_wa(0)
+        first_product(0)
+        round_wa(1)
+        first_product(1)
+        empty_h(0)
+        round_wa(2)
+        quantise_h(0, "wa_raw2_0", skip=4096)
+        first_product(2)
+        empty_h(1)
+        round_wa(3)
+        deal_packed(0)
+        quantise_h(1, None)
+        first_product(3)
+        empty_h(2)
+        deal_packed(1)
+        quantise_h(2, "wb_raw1")
+        second_product(0)
+        empty_y(0)
+        empty_h(3)
+        deal_packed(2)
+        second_product(1)
+        round_y_all(0)
+        deal_packed(3)
+        quantise_h(3, "wb_raw3")
+        empty_y(1)
+        quantise_y(0)
+        second_product(2)
+        round_y_all(1)
+        empty_y(2)
+        quantise_y(1)
+        second_product(3)
+        round_y_all(2)
+        empty_y(3)
+        quantise_y(2)
+        round_y_all(3)
+        quantise_y(3)
 
         for q in range(QUADRANTS):
             queue = nc.sync if q % 2 == 0 else nc.scalar

@@ -77,10 +77,10 @@ def tile_moe_elr_s_relu_kernel(tc, x_words, x_scales, w_words, w_scales, wa, wb_
             wb_raw[e] = sbuf("wb_raw%d" % e, [P, N], I32)
             nc.sync.dma_start(out=wb_raw[e][:], in_=wb_words[e, 0].rearrange("p n d -> p (n d)").bitcast(I32))
 
-        def deal(dst, src, count=1):
+        def deal(dst, src):
             nc.vector.tensor_copy(
-                out=dst.rearrange("p (e t m) -> p e m t", e=count, t=PACK),
-                in_=src.rearrange("p (e m t) -> p e m t", e=count, t=PACK),
+                out=dst.rearrange("p (a b m) -> p a m b", a=2, b=2),
+                in_=src.rearrange("p (m a b) -> p a m b", a=2, b=2),
             )
 
         dealt_s = {}
@@ -129,14 +129,14 @@ def tile_moe_elr_s_relu_kernel(tc, x_words, x_scales, w_words, w_scales, wa, wb_
 
         def round_wa(e):
             wa_bf[e] = sbuf("wa_bf%d" % e, [P, PACK * H], BF16)
-            dst = wa_bf[e][:].rearrange("p (t m j) -> p m j t", t=PACK, j=PACK)
+            dst = wa_bf[e][:].rearrange("p (a b m j) -> p a m j b", a=2, b=2, j=PACK)
             groups = P // WA_PARTS[e]
             for a in range(WA_PARTS[e]):
-                src = wa_raw[(e, a)][:].rearrange("p j (m t) -> p m j t", t=PACK)
+                src = wa_raw[(e, a)][:].rearrange("p j (m a b) -> p a m j b", a=2, b=2)
                 cut = groups - VECTOR_GROUPS[e] if a == WA_PARTS[e] - 1 else groups
-                nc.scalar.copy(out=dst[:, a * groups:a * groups + cut], in_=src[:, 0:cut])
+                nc.scalar.copy(out=dst[:, :, a * groups:a * groups + cut], in_=src[:, :, 0:cut])
                 if cut < groups:
-                    nc.vector.tensor_copy(out=dst[:, a * groups + cut:(a + 1) * groups], in_=src[:, cut:groups])
+                    nc.vector.tensor_copy(out=dst[:, :, a * groups + cut:(a + 1) * groups], in_=src[:, :, cut:groups])
 
         def first_product(e):
             wa_w = sbuf("wa_w%d" % e, [P, H], U32, over="wb_raw0" if e == E - 1 else None)

@@ -25,7 +25,7 @@ BANKS = 4
 LINE = 4
 WINDOW = 1536
 WA_PARTS = (2, 1, 1, 1)
-VECTOR_GROUPS = (0, 64, 96, 48)
+VECTOR_GROUPS = (0, 64, 96, 96)
 
 
 def tile_moe_elr_s_relu_kernel(tc, x_words, x_scales, w_words, w_scales, wa, wb_words, wb_scales, offs, out_0, out_1, out_2):
@@ -39,13 +39,13 @@ def tile_moe_elr_s_relu_kernel(tc, x_words, x_scales, w_words, w_scales, wa, wb_
         start = {}
         used = [0]
 
-        def sbuf(name, shape, dtype, over=None, skip=0):
+        def sbuf(name, shape, dtype, over=None, skip=0, room=0):
             if over is None:
                 start[name] = sum(used)
                 size = ITEM_BYTES[dtype]
                 for extent in shape[1:]:
                     size = size * extent
-                used.append(size)
+                used.append(max(size, room))
             else:
                 start[name] = start[over] + skip
             return work.tile(shape, dtype, name=name, tag=name, align_bytes=64, offset=start[name])
@@ -53,7 +53,7 @@ def tile_moe_elr_s_relu_kernel(tc, x_words, x_scales, w_words, w_scales, wa, wb_
         offsets = keep.tile([P, E * C // 16], U16, name="offsets")
         x_w = sbuf("x_w", [P, WINDOW], I32)
         x_s = sbuf("x_s", [P, WINDOW], U8)
-        s_raw = sbuf("s_raw", [P, N], U8)
+        s_raw = sbuf("s_raw", [P, N], U8, room=PACK * H)
         w_s = sbuf("w_s", [P, E * N], U8)
         nc.vector.memset(x_s[:, 0:T].bitcast(I32), 0)
         nc.vector.memset(w_s[:].bitcast(I32), 0)
@@ -109,9 +109,10 @@ def tile_moe_elr_s_relu_kernel(tc, x_words, x_scales, w_words, w_scales, wa, wb_
         for q in range(QUADRANTS):
             nc.sync.dma_start(out=s_raw[32 * q:32 * q + 4 * E, :].bitcast(I32), in_=wb_scales[:, 0, 4 * q:4 * q + 4, :].bitcast(I32))
         load_wa(2)
+        load_packed(0)
         load_wa(3)
         deal_scales()
-        for e in range(E):
+        for e in range(1, E):
             load_packed(e)
 
         slot_w = sbuf("slot_w", [P, E * C], U32)
@@ -139,7 +140,7 @@ def tile_moe_elr_s_relu_kernel(tc, x_words, x_scales, w_words, w_scales, wa, wb_
                     nc.vector.tensor_copy(out=dst[:, :, a * groups + cut:(a + 1) * groups], in_=src[:, :, cut:groups])
 
         def first_product(e):
-            wa_w = sbuf("wa_w%d" % e, [P, H], U32, over="wb_raw0" if e == E - 1 else None)
+            wa_w = sbuf("wa_w%d" % e, [P, H], U32, over={1: "s_raw", 3: "wb_raw1"}.get(e))
             wa_s = sbuf("wa_s%d" % e, [P, H], U8)
             nc.vector.quantize_mx(out=wa_w[:].bitcast(FP8X4), scales=wa_s[:], in_=wa_bf[e][:])
             for b in banks:
@@ -158,7 +159,7 @@ def tile_moe_elr_s_relu_kernel(tc, x_words, x_scales, w_words, w_scales, wa, wb_
         h_s = {}
 
         def empty_h(e):
-            h_bf[e] = sbuf("h_bf%d" % e, [P, PACK * C], BF16, over="wa_raw%d_0" % (e + 1) if e + 1 < E else None)
+            h_bf[e] = sbuf("h_bf%d" % e, [P, PACK * C], BF16, over="wa_raw%d_0" % (e + 1) if e < 2 else None)
             for b in banks:
                 nc.scalar.activation(
                     out=h_bf[e][:, span(b, PACK * BANK_SLOTS)].rearrange("p (u t) -> p u t", t=PACK),
@@ -166,8 +167,8 @@ def tile_moe_elr_s_relu_kernel(tc, x_words, x_scales, w_words, w_scales, wa, wb_
                     func=RELU,
                 )
 
-        def quantise_h(e, over, skip=0):
-            h_w[e] = sbuf("h_w%d" % e, [P, C], U32, over=over, skip=skip)
+        def quantise_h(e):
+            h_w[e] = sbuf("h_w%d" % e, [P, C], U32, over="wb_raw%d" % e if e % 2 == 0 else None)
             h_s[e] = sbuf("h_s%d" % e, [P, C], U8)
             width = BANK_SLOTS if e == E - 1 else C
             for piece in range(C // width):
@@ -182,9 +183,7 @@ def tile_moe_elr_s_relu_kernel(tc, x_words, x_scales, w_words, w_scales, wa, wb_
         y_s = sbuf("y_s", [P, E * C], U8)
         w_w = {}
         wb_w = {}
-        y_acc = {}
         y_f = {}
-        y_bf = {}
 
         def deal_packed(e):
             w_w[e] = sbuf("w_w%d" % e, [P, 2 * N], U8)
@@ -193,90 +192,62 @@ def tile_moe_elr_s_relu_kernel(tc, x_words, x_scales, w_words, w_scales, wa, wb_
             deal(wb_w[e][:], wb_raw[e][:])
 
         def second_product(e):
+            y_f[e] = sbuf("y_f%d" % e, [P, PACK, C], F32)
+            last = e == E - 1
             for b in banks:
-                own = span(b, BANK_SLOTS)
-                slots = span(e * len(banks) + b, BANK_SLOTS)
                 acc = psum_y.tile([P, PACK, BANK_SLOTS], F32, name="acc_y")
-                y_acc[(e, b)] = acc
-                for t in range(PACK):
+                for g in range(PACK):
+                    t, half = (g, b) if last else (2 * b + g // 2, g % 2)
+                    own = span(half, BANK_SLOTS)
+                    slots = span(e * len(banks) + half, BANK_SLOTS)
                     nc.tensor.matmul_mx(
-                        out=acc[:, t, :],
+                        out=acc[:, g, :],
                         lhsT=w_w[e][:, span(t, 2 * P)].bitcast(FP4X4), lhsT_scale=dealt_s["w"][:, span(e * PACK + t, P)],
                         rhs=slot_w[:, slots].bitcast(FP8X4), rhs_scale=slot_s[:, slots],
                         start=True, stop=False,
                     )
                     nc.tensor.matmul_mx(
-                        out=acc[:, t, :],
+                        out=acc[:, g, :],
                         lhsT=wb_w[e][:, span(t, P)].bitcast(FP8X4), lhsT_scale=dealt_s["wb"][4 * e:P, span(t, P)],
                         rhs=h_w[e][:, own].bitcast(FP8X4), rhs_scale=h_s[e][:, own],
                         start=False, stop=True,
                     )
-
-        def empty_y(e):
-            y_f[e] = sbuf("y_f%d" % e, [P, PACK, C], F32)
-            for b in banks:
-                nc.scalar.copy(out=y_f[e][:, :, span(b, BANK_SLOTS)], in_=y_acc[(e, b)][:])
-            nc.sync.dma_start(out=out_rows[:, :, span(e, C)], in_=y_f[e][:])
-
-        def round_y(e, b):
-            if b == 0:
-                y_bf[e] = sbuf("y_bf%d" % e, [P, PACK * C], BF16)
-            nc.vector.tensor_copy(
-                out=y_bf[e][:, span(b, PACK * BANK_SLOTS)].rearrange("p (c i t) -> p c t i", i=LINE, t=PACK),
-                in_=y_f[e][:, :, span(b, BANK_SLOTS)].rearrange("p t (c i) -> p c t i", i=LINE),
-            )
+                if last:
+                    nc.scalar.copy(out=y_f[e][:, :, span(b, BANK_SLOTS)], in_=acc[:])
+                else:
+                    nc.scalar.copy(out=y_f[e][:, span(b, 2), :].rearrange("p t c -> p (t c)"), in_=acc[:].rearrange("p g u -> p (g u)"))
+                    nc.sync.dma_start(out=out_rows[:, span(b, 2), span(e, C)], in_=y_f[e][:, span(b, 2), :])
+            if last:
+                nc.sync.dma_start(out=out_rows[:, :, span(e, C)], in_=y_f[e][:])
 
         def quantise_y(e):
+            y_bf = sbuf("y_bf%d" % e, [P, PACK * C], BF16)
             y_w = sbuf("y_w%d" % e, [P, C], U32)
             width = BANK_SLOTS if e == E - 1 else C
             for piece in range(C // width):
+                nc.vector.tensor_copy(
+                    out=y_bf[:, span(piece, PACK * width)].rearrange("p (c i t) -> p c t i", i=LINE, t=PACK),
+                    in_=y_f[e][:, :, span(piece, width)].rearrange("p t (c i) -> p c t i", i=LINE),
+                )
                 nc.vector.quantize_mx(
                     out=y_w[:, span(piece, width)].bitcast(FP8X4),
                     scales=y_s[:, e * C + piece * width:e * C + (piece + 1) * width],
-                    in_=y_bf[e][:, span(piece, PACK * width)],
+                    in_=y_bf[:, span(piece, PACK * width)],
                 )
             nc.sync.dma_start(out=out_words[:, span(e, C)], in_=y_w[:].bitcast(I32))
 
-        def round_y_all(e):
-            for b in banks:
-                round_y(e, b)
-
-        round_wa(0)
-        first_product(0)
-        round_wa(1)
-        first_product(1)
-        empty_h(0)
-        round_wa(2)
-        quantise_h(0, "wa_raw2_0", skip=4096)
-        first_product(2)
-        empty_h(1)
-        round_wa(3)
-        deal_packed(0)
-        quantise_h(1, None)
-        first_product(3)
-        empty_h(2)
-        deal_packed(1)
-        quantise_h(2, "wb_raw1")
-        second_product(0)
-        empty_y(0)
-        empty_h(3)
-        deal_packed(2)
-        second_product(1)
-        round_y_all(0)
-        deal_packed(3)
-        quantise_h(3, "wb_raw3")
-        empty_y(1)
-        quantise_y(0)
-        second_product(2)
-        round_y_all(1)
-        empty_y(2)
-        quantise_y(1)
-        second_product(3)
-        round_y_all(2)
-        empty_y(3)
-        quantise_y(2)
-        round_y_all(3)
-        quantise_y(3)
+        for step in range(E + 3):
+            if step < E:
+                round_wa(step)
+                first_product(step)
+            if 0 <= step - 2 < E:
+                second_product(step - 2)
+            if 0 <= step - 1 < E:
+                empty_h(step - 1)
+                deal_packed(step - 1)
+                quantise_h(step - 1)
+            if 0 <= step - 3 < E:
+                quantise_y(step - 3)
 
         for q in range(QUADRANTS):
             queue = nc.sync if q % 2 == 0 else nc.scalar

@@ -24,8 +24,8 @@ BANK_SLOTS = 128
 BANKS = 4
 LINE = 4
 WINDOW = 1536
-WA_PARTS = (2, 1, 1, 1)
-VECTOR_GROUPS = (0, 64, 96, 96)
+WA_PARTS = (1, 1, 1, 1)
+VECTOR_GROUPS = (0, 64, 96, 80)
 
 
 def tile_moe_elr_s_relu_kernel(tc, x_words, x_scales, w_words, w_scales, wa, wb_words, wb_scales, offs, out_0, out_1, out_2):
@@ -180,7 +180,7 @@ def tile_moe_elr_s_relu_kernel(tc, x_words, x_scales, w_words, w_scales, wa, wb_
 
         out_rows = out_0.rearrange("(p t) j -> p t j", t=PACK)
         out_words = out_1[0].rearrange("p j d -> p (j d)").bitcast(I32)
-        y_s = sbuf("y_s", [P, E * C], U8)
+        y_s = sbuf("y_s", [P, C], U8)
         w_w = {}
         wb_w = {}
         y_f = {}
@@ -231,7 +231,7 @@ def tile_moe_elr_s_relu_kernel(tc, x_words, x_scales, w_words, w_scales, wa, wb_
                 )
                 nc.vector.quantize_mx(
                     out=y_w[:, span(piece, width)].bitcast(FP8X4),
-                    scales=y_s[:, e * C + piece * width:e * C + (piece + 1) * width],
+                    scales=y_s[4 * e:P, span(piece, width)],
                     in_=y_bf[:, span(piece, PACK * width)],
                 )
             nc.sync.dma_start(out=out_words[:, span(e, C)], in_=y_w[:].bitcast(I32))
@@ -251,4 +251,7 @@ def tile_moe_elr_s_relu_kernel(tc, x_words, x_scales, w_words, w_scales, wa, wb_
 
         for q in range(QUADRANTS):
             queue = nc.sync if q % 2 == 0 else nc.scalar
-            queue.dma_start(out=out_2[0, 4 * q:4 * q + 4, :].bitcast(I32), in_=y_s[32 * q:32 * q + 4, :].bitcast(I32))
+            queue.dma_start(
+                out=out_2[0, 4 * q:4 * q + 4, :].bitcast(I32).rearrange("r (e c) -> e r c", e=E),
+                in_=y_s[32 * q:32 * q + 4 * E, :].bitcast(I32),
+            )

@@ -24,8 +24,8 @@ BANK_SLOTS = 128
 BANKS = 4
 LINE = 4
 WINDOW = 1536
-WA_PARTS = (1, 1, 1, 1)
-VECTOR_GROUPS = (0, 64, 96, 80)
+WA_PARTS = (2, 1, 1, 1)
+VECTOR_GROUPS = (0, 32, 64, 64)
 
 
 def tile_moe_elr_s_relu_kernel(tc, x_words, x_scales, w_words, w_scales, wa, wb_words, wb_scales, offs, out_0, out_1, out_2):
@@ -108,8 +108,8 @@ def tile_moe_elr_s_relu_kernel(tc, x_words, x_scales, w_words, w_scales, wa, wb_
         load_wa(1)
         for q in range(QUADRANTS):
             nc.sync.dma_start(out=s_raw[32 * q:32 * q + 4 * E, :].bitcast(I32), in_=wb_scales[:, 0, 4 * q:4 * q + 4, :].bitcast(I32))
-        load_wa(2)
         load_packed(0)
+        load_wa(2)
         load_wa(3)
         deal_scales()
         for e in range(1, E):
@@ -168,7 +168,7 @@ def tile_moe_elr_s_relu_kernel(tc, x_words, x_scales, w_words, w_scales, wa, wb_
                 )
 
         def quantise_h(e):
-            h_w[e] = sbuf("h_w%d" % e, [P, C], U32, over="wb_raw%d" % e if e % 2 == 0 else None)
+            h_w[e] = sbuf("h_w%d" % e, [P, C], U32, over="wb_raw2" if e == 2 else None)
             h_s[e] = sbuf("h_s%d" % e, [P, C], U8)
             width = BANK_SLOTS if e == E - 1 else C
             for piece in range(C // width):
@@ -180,10 +180,11 @@ def tile_moe_elr_s_relu_kernel(tc, x_words, x_scales, w_words, w_scales, wa, wb_
 
         out_rows = out_0.rearrange("(p t) j -> p t j", t=PACK)
         out_words = out_1[0].rearrange("p j d -> p (j d)").bitcast(I32)
-        y_s = sbuf("y_s", [P, C], U8)
+        y_s = sbuf("y_s", [P, E * C], U8)
         w_w = {}
         wb_w = {}
         y_f = {}
+        last_acc = []
 
         def deal_packed(e):
             w_w[e] = sbuf("w_w%d" % e, [P, 2 * N], U8)
@@ -219,19 +220,26 @@ def tile_moe_elr_s_relu_kernel(tc, x_words, x_scales, w_words, w_scales, wa, wb_
                     nc.sync.dma_start(out=out_rows[:, span(b, 2), span(e, C)], in_=y_f[e][:, span(b, 2), :])
             if last:
                 nc.sync.dma_start(out=out_rows[:, :, span(e, C)], in_=y_f[e][:])
+                last_acc.append(acc)
 
         def quantise_y(e):
             y_bf = sbuf("y_bf%d" % e, [P, PACK * C], BF16)
             y_w = sbuf("y_w%d" % e, [P, C], U32)
             width = BANK_SLOTS if e == E - 1 else C
             for piece in range(C // width):
-                nc.vector.tensor_copy(
-                    out=y_bf[:, span(piece, PACK * width)].rearrange("p (c i t) -> p c t i", i=LINE, t=PACK),
-                    in_=y_f[e][:, :, span(piece, width)].rearrange("p t (c i) -> p c t i", i=LINE),
-                )
+                if e == E - 1 and piece == 1:
+                    nc.scalar.copy(
+                        out=y_bf[:, span(piece, PACK * width)].rearrange("p (u t) -> p u t", t=PACK),
+                        in_=last_acc[0][:].rearrange("p t u -> p u t"),
+                    )
+                else:
+                    nc.vector.tensor_copy(
+                        out=y_bf[:, span(piece, PACK * width)].rearrange("p (c i t) -> p c t i", i=LINE, t=PACK),
+                        in_=y_f[e][:, :, span(piece, width)].rearrange("p t (c i) -> p c t i", i=LINE),
+                    )
                 nc.vector.quantize_mx(
                     out=y_w[:, span(piece, width)].bitcast(FP8X4),
-                    scales=y_s[4 * e:P, span(piece, width)],
+                    scales=y_s[:, e * C + piece * width:e * C + (piece + 1) * width],
                     in_=y_bf[:, span(piece, PACK * width)],
                 )
             nc.sync.dma_start(out=out_words[:, span(e, C)], in_=y_w[:].bitcast(I32))
@@ -251,7 +259,4 @@ def tile_moe_elr_s_relu_kernel(tc, x_words, x_scales, w_words, w_scales, wa, wb_
 
         for q in range(QUADRANTS):
             queue = nc.sync if q % 2 == 0 else nc.scalar
-            queue.dma_start(
-                out=out_2[0, 4 * q:4 * q + 4, :].bitcast(I32).rearrange("r (e c) -> e r c", e=E),
-                in_=y_s[32 * q:32 * q + 4 * E, :].bitcast(I32),
-            )
+            queue.dma_start(out=out_2[0, 4 * q:4 * q + 4, :].bitcast(I32), in_=y_s[32 * q:32 * q + 4, :].bitcast(I32))

@@ -25,7 +25,7 @@ BANKS = 4
 LINE = 4
 WINDOW = 1536
 WA_PARTS = (2, 1, 1, 1)
-VECTOR_GROUPS = (0, 32, 64, 64)
+VECTOR_GROUPS = (0, 64, 96, 96)
 
 
 def tile_moe_elr_s_relu_kernel(tc, x_words, x_scales, w_words, w_scales, wa, wb_words, wb_scales, offs, out_0, out_1, out_2):
@@ -108,8 +108,8 @@ def tile_moe_elr_s_relu_kernel(tc, x_words, x_scales, w_words, w_scales, wa, wb_
         load_wa(1)
         for q in range(QUADRANTS):
             nc.sync.dma_start(out=s_raw[32 * q:32 * q + 4 * E, :].bitcast(I32), in_=wb_scales[:, 0, 4 * q:4 * q + 4, :].bitcast(I32))
-        load_packed(0)
         load_wa(2)
+        load_packed(0)
         load_wa(3)
         deal_scales()
         for e in range(1, E):
@@ -168,7 +168,7 @@ def tile_moe_elr_s_relu_kernel(tc, x_words, x_scales, w_words, w_scales, wa, wb_
                 )
 
         def quantise_h(e):
-            h_w[e] = sbuf("h_w%d" % e, [P, C], U32, over="wb_raw2" if e == 2 else None)
+            h_w[e] = sbuf("h_w%d" % e, [P, C], U32, over="wb_raw%d" % e if e % 2 == 0 else None)
             h_s[e] = sbuf("h_s%d" % e, [P, C], U8)
             width = BANK_SLOTS if e == E - 1 else C
             for piece in range(C // width):
@@ -215,11 +215,11 @@ def tile_moe_elr_s_relu_kernel(tc, x_words, x_scales, w_words, w_scales, wa, wb_
                     )
                 if last:
                     nc.scalar.copy(out=y_f[e][:, :, span(b, BANK_SLOTS)], in_=acc[:])
+                    nc.sync.dma_start(out=out_rows[:, :, span(e * len(banks) + b, BANK_SLOTS)], in_=y_f[e][:, :, span(b, BANK_SLOTS)])
                 else:
                     nc.scalar.copy(out=y_f[e][:, span(b, 2), :].rearrange("p t c -> p (t c)"), in_=acc[:].rearrange("p g u -> p (g u)"))
                     nc.sync.dma_start(out=out_rows[:, span(b, 2), span(e, C)], in_=y_f[e][:, span(b, 2), :])
             if last:
-                nc.sync.dma_start(out=out_rows[:, :, span(e, C)], in_=y_f[e][:])
                 last_acc.append(acc)
 
         def quantise_y(e):

@@ -24,8 +24,9 @@ BANK_SLOTS = 128
 BANKS = 4
 LINE = 4
 WINDOW = 1536
-WA_PARTS = (2, 1, 1, 1)
-VECTOR_GROUPS = (0, 64, 96, 96)
+WA_PARTS = (1, 1, 1, 2)
+VECTOR_GROUPS = ((24,), (64,), (96,), (32, 48))
+WB_ROWS = 4
 
 
 def tile_moe_elr_s_relu_kernel(tc, x_words, x_scales, w_words, w_scales, wa, wb_words, wb_scales, offs, out_0, out_1, out_2):
@@ -39,24 +40,26 @@ def tile_moe_elr_s_relu_kernel(tc, x_words, x_scales, w_words, w_scales, wa, wb_
         start = {}
         used = [0]
 
-        def sbuf(name, shape, dtype, over=None, skip=0, room=0):
+        def sbuf(name, shape, dtype, over=None):
             if over is None:
                 start[name] = sum(used)
                 size = ITEM_BYTES[dtype]
                 for extent in shape[1:]:
                     size = size * extent
-                used.append(max(size, room))
+                used.append(size)
             else:
-                start[name] = start[over] + skip
+                start[name] = start[over]
             return work.tile(shape, dtype, name=name, tag=name, align_bytes=64, offset=start[name])
+
+        def span(index, width):
+            return slice(index * width, (index + 1) * width)
 
         offsets = keep.tile([P, E * C // 16], U16, name="offsets")
         x_w = sbuf("x_w", [P, WINDOW], I32)
         x_s = sbuf("x_s", [P, WINDOW], U8)
-        s_raw = sbuf("s_raw", [P, N], U8, room=PACK * H)
-        w_s = sbuf("w_s", [P, E * N], U8)
+        s_raw = sbuf("s_raw", [P, E * N], U8)
         nc.vector.memset(x_s[:, 0:T].bitcast(I32), 0)
-        nc.vector.memset(w_s[:].bitcast(I32), 0)
+        nc.vector.memset(s_raw[:].bitcast(I32), 0)
         nc.vector.memset(x_w[:, T:WINDOW], 0)
         nc.vector.memset(x_s[:, T:WINDOW].bitcast(I32), 0)
 
@@ -64,56 +67,43 @@ def tile_moe_elr_s_relu_kernel(tc, x_words, x_scales, w_words, w_scales, wa, wb_
         w_raw = {}
         wb_raw = {}
 
-        def load_wa(e):
+        def load_wa(e, part):
             width = H // WA_PARTS[e]
             rows = wa[e].rearrange("(p j) c -> p j c", j=PACK)
-            for a in range(WA_PARTS[e]):
-                wa_raw[(e, a)] = sbuf("wa_raw%d_%d" % (e, a), [P, PACK, width], F32)
-                nc.sync.dma_start(out=wa_raw[(e, a)][:], in_=rows[:, :, a * width:(a + 1) * width])
+            wa_raw[(e, part)] = sbuf("wa_raw%d_%d" % (e, part), [P, PACK, width], F32)
+            nc.sync.dma_start(out=wa_raw[(e, part)][:], in_=rows[:, :, span(part, width)])
 
-        def load_packed(e):
-            w_raw[e] = sbuf("w_raw%d" % e, [P, N // 2], I32)
-            nc.sync.dma_start(out=w_raw[e][:], in_=w_words[e, 0].bitcast(I32))
+        def load_w(pair):
+            w_raw[pair] = sbuf("w_raw%d" % pair, [P, 2, N // 2], I32)
+            nc.sync.dma_start(out=w_raw[pair][:], in_=w_words[span(pair, 2), 0].bitcast(I32).rearrange("e p c -> p e c"))
+
+        def load_wb(e):
             wb_raw[e] = sbuf("wb_raw%d" % e, [P, N], I32)
             nc.sync.dma_start(out=wb_raw[e][:], in_=wb_words[e, 0].rearrange("p n d -> p (n d)").bitcast(I32))
 
-        def deal(dst, src):
-            nc.vector.tensor_copy(
-                out=dst.rearrange("p (a b m) -> p a m b", a=2, b=2),
-                in_=src.rearrange("p (m a b) -> p a m b", a=2, b=2),
-            )
-
-        dealt_s = {}
-
-        def deal_scales():
-            dealt_s["wb"] = sbuf("s_dealt", [P, N], U8)
-            deal(dealt_s["wb"][:], s_raw[:])
-            dealt_s["w"] = w_s
-            for q in range(QUADRANTS):
+        def load_scales(scales, first):
+            for r in range(QUADRANTS):
                 nc.sync.dma_start(
-                    out=w_s[32 * q:32 * q + 4, :].bitcast(I32).rearrange("r (e c) -> r e c", e=E),
-                    in_=dealt_s["wb"][32 * q + 16:32 * q + 32, :].bitcast(I32),
+                    out=s_raw[first + r:P:32, :].bitcast(I32).rearrange("q (e c) -> q e c", e=E),
+                    in_=scales[:, 0, r:16:4, :].bitcast(I32).rearrange("e q c -> q e c"),
                 )
 
         nc.sync.dma_start(out=x_w[:, 0:T], in_=x_words[0].rearrange("p t d -> p (t d)").bitcast(I32))
         nc.sync.dma_start(offsets[:], offs)
-        for q in range(QUADRANTS):
-            nc.sync.dma_start(out=x_s[32 * q:32 * q + 4, 0:T].bitcast(I32), in_=x_scales[0, 4 * q:4 * q + 4, :].bitcast(I32))
-        load_wa(0)
-        for q in range(QUADRANTS):
-            nc.sync.dma_start(
-                out=s_raw[32 * q + 16:32 * q + 32, :].bitcast(I32),
-                in_=w_scales[:, 0, 4 * q:4 * q + 4, :].bitcast(I32).rearrange("e r c -> r e c"),
-            )
-        load_wa(1)
-        for q in range(QUADRANTS):
-            nc.sync.dma_start(out=s_raw[32 * q:32 * q + 4 * E, :].bitcast(I32), in_=wb_scales[:, 0, 4 * q:4 * q + 4, :].bitcast(I32))
-        load_wa(2)
-        load_packed(0)
-        load_wa(3)
-        deal_scales()
-        for e in range(1, E):
-            load_packed(e)
+        for r in range(QUADRANTS):
+            nc.sync.dma_start(out=x_s[r:P:32, 0:T].bitcast(I32), in_=x_scales[0, r:16:4, :].bitcast(I32))
+        for e in range(E - 1):
+            load_wa(e, 0)
+        load_w(0)
+        load_wb(0)
+        load_scales(w_scales, 0)
+        load_wa(E - 1, 0)
+        load_scales(wb_scales, WB_ROWS)
+        load_wb(1)
+        load_wa(E - 1, 1)
+        load_wb(2)
+        load_w(1)
+        load_wb(3)
 
         slot_w = sbuf("slot_w", [P, E * C], U32)
         slot_s = sbuf("slot_s", [P, E * C], U8)
@@ -122,27 +112,21 @@ def tile_moe_elr_s_relu_kernel(tc, x_words, x_scales, w_words, w_scales, wa, wb_
 
         banks = range(C // BANK_SLOTS)
 
-        def span(index, width):
-            return slice(index * width, (index + 1) * width)
-
-        wa_bf = {}
         h_acc = {}
-
-        def round_wa(e):
-            wa_bf[e] = sbuf("wa_bf%d" % e, [P, PACK * H], BF16)
-            dst = wa_bf[e][:].rearrange("p (a b m j) -> p a m j b", a=2, b=2, j=PACK)
-            groups = P // WA_PARTS[e]
-            for a in range(WA_PARTS[e]):
-                src = wa_raw[(e, a)][:].rearrange("p j (m a b) -> p a m j b", a=2, b=2)
-                cut = groups - VECTOR_GROUPS[e] if a == WA_PARTS[e] - 1 else groups
-                nc.scalar.copy(out=dst[:, :, a * groups:a * groups + cut], in_=src[:, :, 0:cut])
-                if cut < groups:
-                    nc.vector.tensor_copy(out=dst[:, :, a * groups + cut:(a + 1) * groups], in_=src[:, :, cut:groups])
+        h_bf = {}
 
         def first_product(e):
-            wa_w = sbuf("wa_w%d" % e, [P, H], U32, over={1: "s_raw", 3: "wb_raw1"}.get(e))
+            wa_bf = sbuf("wa_bf%d" % e, [P, PACK * H], BF16)
+            dst = wa_bf[:].rearrange("p (a b m j) -> p a m j b", a=2, b=2, j=PACK)
+            groups = P // WA_PARTS[e]
+            for part in range(WA_PARTS[e]):
+                src = wa_raw[(e, part)][:].rearrange("p j (m a b) -> p a m j b", a=2, b=2)
+                cut = groups - VECTOR_GROUPS[e][part]
+                nc.scalar.copy(out=dst[:, :, part * groups:part * groups + cut], in_=src[:, :, 0:cut])
+                nc.vector.tensor_copy(out=dst[:, :, part * groups + cut:(part + 1) * groups], in_=src[:, :, cut:groups])
+            wa_w = sbuf("wa_w%d" % e, [P, H], U32)
             wa_s = sbuf("wa_s%d" % e, [P, H], U8)
-            nc.vector.quantize_mx(out=wa_w[:].bitcast(FP8X4), scales=wa_s[:], in_=wa_bf[e][:])
+            nc.vector.quantize_mx(out=wa_w[:].bitcast(FP8X4), scales=wa_s[:], in_=wa_bf[:])
             for b in banks:
                 slots = span(e * len(banks) + b, BANK_SLOTS)
                 h_acc[(e, b)] = psum_h.tile([P, PACK, BANK_SLOTS], F32, name="acc_h")
@@ -154,12 +138,8 @@ def tile_moe_elr_s_relu_kernel(tc, x_words, x_scales, w_words, w_scales, wa, wb_
                         start=True, stop=True,
                     )
 
-        h_bf = {}
-        h_w = {}
-        h_s = {}
-
         def empty_h(e):
-            h_bf[e] = sbuf("h_bf%d" % e, [P, PACK * C], BF16, over="wa_raw%d_0" % (e + 1) if e < 2 else None)
+            h_bf[e] = sbuf("h_bf%d" % e, [P, PACK * C], BF16)
             for b in banks:
                 nc.scalar.activation(
                     out=h_bf[e][:, span(b, PACK * BANK_SLOTS)].rearrange("p (u t) -> p u t", t=PACK),
@@ -167,8 +147,45 @@ def tile_moe_elr_s_relu_kernel(tc, x_words, x_scales, w_words, w_scales, wa, wb_
                     func=RELU,
                 )
 
+        for e in range(E):
+            first_product(e)
+            if e > 0:
+                empty_h(e - 1)
+        empty_h(E - 1)
+
+        def deal(dst, src):
+            nc.vector.tensor_copy(
+                out=dst.rearrange("p e (a b m) -> p a e m b", a=2, b=2),
+                in_=src.rearrange("p e (m a b) -> p a e m b", a=2, b=2),
+            )
+
+        w_w = {}
+        wb_w = {}
+        s_dealt = {}
+        h_w = {}
+        h_s = {}
+        y_acc = {}
+        y_f = {}
+        y_bf = {}
+
+        def deal_w(pair):
+            dealt = sbuf("w_w%d" % pair, [P, 2, 2 * N], U8)
+            deal(dealt[:].bitcast(U16), w_raw[pair][:].bitcast(U16))
+            for k in range(2):
+                w_w[2 * pair + k] = dealt[:, k, :]
+
+        def deal_scales(first, count):
+            dealt = sbuf("s_dealt%d" % first, [P, count, N], U8)
+            deal(dealt[:], s_raw[:, first * N:(first + count) * N].rearrange("p (e c) -> p e c", e=count))
+            for k in range(count):
+                s_dealt[first + k] = dealt[:, k, :]
+
+        def deal_wb(e):
+            wb_w[e] = sbuf("wb_w%d" % e, [P, 1, N], I32)
+            deal(wb_w[e][:], wb_raw[e][:].rearrange("p (e c) -> p e c", e=1))
+
         def quantise_h(e):
-            h_w[e] = sbuf("h_w%d" % e, [P, C], U32, over="wb_raw%d" % e if e % 2 == 0 else None)
+            h_w[e] = sbuf("h_w%d" % e, [P, C], U32, over={0: "w_raw0", 2: "s_raw"}.get(e))
             h_s[e] = sbuf("h_s%d" % e, [P, C], U8)
             width = BANK_SLOTS if e == E - 1 else C
             for piece in range(C // width):
@@ -178,85 +195,89 @@ def tile_moe_elr_s_relu_kernel(tc, x_words, x_scales, w_words, w_scales, wa, wb_
                     in_=h_bf[e][:, span(piece, PACK * width)],
                 )
 
-        out_rows = out_0.rearrange("(p t) j -> p t j", t=PACK)
-        out_words = out_1[0].rearrange("p j d -> p (j d)").bitcast(I32)
-        y_s = sbuf("y_s", [P, E * C], U8)
-        w_w = {}
-        wb_w = {}
-        y_f = {}
-        last_acc = []
-
-        def deal_packed(e):
-            w_w[e] = sbuf("w_w%d" % e, [P, 2 * N], U8)
-            wb_w[e] = sbuf("wb_w%d" % e, [P, N], I32)
-            deal(w_w[e][:].bitcast(U16), w_raw[e][:].bitcast(U16))
-            deal(wb_w[e][:], wb_raw[e][:])
-
         def second_product(e):
-            y_f[e] = sbuf("y_f%d" % e, [P, PACK, C], F32)
             last = e == E - 1
             for b in banks:
                 acc = psum_y.tile([P, PACK, BANK_SLOTS], F32, name="acc_y")
+                y_acc[(e, b)] = acc
                 for g in range(PACK):
                     t, half = (g, b) if last else (2 * b + g // 2, g % 2)
                     own = span(half, BANK_SLOTS)
                     slots = span(e * len(banks) + half, BANK_SLOTS)
                     nc.tensor.matmul_mx(
                         out=acc[:, g, :],
-                        lhsT=w_w[e][:, span(t, 2 * P)].bitcast(FP4X4), lhsT_scale=dealt_s["w"][:, span(e * PACK + t, P)],
+                        lhsT=w_w[e][:, span(t, 2 * P)].bitcast(FP4X4), lhsT_scale=s_dealt[e][:, span(t, P)],
                         rhs=slot_w[:, slots].bitcast(FP8X4), rhs_scale=slot_s[:, slots],
                         start=True, stop=False,
                     )
                     nc.tensor.matmul_mx(
                         out=acc[:, g, :],
-                        lhsT=wb_w[e][:, span(t, P)].bitcast(FP8X4), lhsT_scale=dealt_s["wb"][4 * e:P, span(t, P)],
+                        lhsT=wb_w[e][:, 0, span(t, P)].bitcast(FP8X4), lhsT_scale=s_dealt[e][WB_ROWS:P, span(t, P)],
                         rhs=h_w[e][:, own].bitcast(FP8X4), rhs_scale=h_s[e][:, own],
                         start=False, stop=True,
                     )
-                if last:
+
+        out_rows = out_0.rearrange("(p t) j -> p t j", t=PACK)
+        out_words = out_1[0].rearrange("p j d -> p (j d)").bitcast(I32)
+        y_w = sbuf("y_w", [P, E * C], U32)
+        y_s = sbuf("y_s", [P, E * C], U8)
+
+        def empty_y(e):
+            y_f[e] = sbuf("y_f%d" % e, [P, PACK, C], F32)
+            y_bf[e] = sbuf("y_bf%d" % e, [P, PACK * C], BF16, over="h_bf3" if e == 1 else None)
+            for b in banks:
+                acc = y_acc[(e, b)]
+                if e == E - 1:
+                    if b == 1:
+                        nc.scalar.copy(
+                            out=y_bf[e][:, span(b, PACK * BANK_SLOTS)].rearrange("p (u t) -> p u t", t=PACK),
+                            in_=acc[:].rearrange("p t u -> p u t"),
+                        )
                     nc.scalar.copy(out=y_f[e][:, :, span(b, BANK_SLOTS)], in_=acc[:])
                     nc.sync.dma_start(out=out_rows[:, :, span(e * len(banks) + b, BANK_SLOTS)], in_=y_f[e][:, :, span(b, BANK_SLOTS)])
                 else:
                     nc.scalar.copy(out=y_f[e][:, span(b, 2), :].rearrange("p t c -> p (t c)"), in_=acc[:].rearrange("p g u -> p (g u)"))
-                    nc.sync.dma_start(out=out_rows[:, span(b, 2), span(e, C)], in_=y_f[e][:, span(b, 2), :])
-            if last:
-                last_acc.append(acc)
+                    if e != 1:
+                        nc.sync.dma_start(out=out_rows[:, span(b, 2), span(e, C)], in_=y_f[e][:, span(b, 2), :])
+            if e == 1:
+                nc.sync.dma_start(out=out_rows[:, :, span(e, C)], in_=y_f[e][:])
+
+        def round_y(e, width):
+            nc.vector.tensor_copy(
+                out=y_bf[e][:, 0:PACK * width].rearrange("p (c i t) -> p c t i", i=LINE, t=PACK),
+                in_=y_f[e][:, :, 0:width].rearrange("p t (c i) -> p c t i", i=LINE),
+            )
 
         def quantise_y(e):
-            y_bf = sbuf("y_bf%d" % e, [P, PACK * C], BF16)
-            y_w = sbuf("y_w%d" % e, [P, C], U32)
             width = BANK_SLOTS if e == E - 1 else C
             for piece in range(C // width):
-                if e == E - 1 and piece == 1:
-                    nc.scalar.copy(
-                        out=y_bf[:, span(piece, PACK * width)].rearrange("p (u t) -> p u t", t=PACK),
-                        in_=last_acc[0][:].rearrange("p t u -> p u t"),
-                    )
-                else:
-                    nc.vector.tensor_copy(
-                        out=y_bf[:, span(piece, PACK * width)].rearrange("p (c i t) -> p c t i", i=LINE, t=PACK),
-                        in_=y_f[e][:, :, span(piece, width)].rearrange("p t (c i) -> p c t i", i=LINE),
-                    )
+                columns = slice(e * C + piece * width, e * C + (piece + 1) * width)
                 nc.vector.quantize_mx(
-                    out=y_w[:, span(piece, width)].bitcast(FP8X4),
-                    scales=y_s[:, e * C + piece * width:e * C + (piece + 1) * width],
-                    in_=y_bf[:, span(piece, PACK * width)],
+                    out=y_w[:, columns].bitcast(FP8X4),
+                    scales=y_s[:, columns],
+                    in_=y_bf[e][:, span(piece, PACK * width)],
                 )
-            nc.sync.dma_start(out=out_words[:, span(e, C)], in_=y_w[:].bitcast(I32))
+            if e != 2:
+                columns = slice(min(e, 2) * C, (e + 1) * C)
+                nc.sync.dma_start(out=out_words[:, columns], in_=y_w[:, columns].bitcast(I32))
 
-        for step in range(E + 3):
-            if step < E:
-                round_wa(step)
-                first_product(step)
-            if 0 <= step - 2 < E:
-                second_product(step - 2)
-            if 0 <= step - 1 < E:
-                empty_h(step - 1)
-                deal_packed(step - 1)
-                quantise_h(step - 1)
-            if 0 <= step - 3 < E:
-                quantise_y(step - 3)
+        for e in range(E):
+            if e % 2 == 0:
+                deal_w(e // 2)
+            if e < 3:
+                deal_scales(e, 1 if e < 2 else 2)
+            deal_wb(e)
+            quantise_h(e)
+            if e >= 2:
+                empty_y(e - 2)
+            second_product(e)
+        empty_y(E - 2)
+        empty_y(E - 1)
+        for e in range(E):
+            round_y(e, BANK_SLOTS if e == E - 1 else C)
+            if e > 0:
+                quantise_y(e - 1)
+        quantise_y(E - 1)
 
-        for q in range(QUADRANTS):
-            queue = nc.sync if q % 2 == 0 else nc.scalar
-            queue.dma_start(out=out_2[0, 4 * q:4 * q + 4, :].bitcast(I32), in_=y_s[32 * q:32 * q + 4, :].bitcast(I32))
+        for r in range(QUADRANTS):
+            nc.scalar.dma_start(out=out_2[0, r:16:4, :].bitcast(I32), in_=y_s[r:P:32, :].bitcast(I32))

@@ -153,10 +153,16 @@ def tile_moe_elr_s_relu_kernel(tc, x_words, x_scales, w_words, w_scales, wa, wb_
                 empty_h(e - 1)
         empty_h(E - 1)
 
-        def deal(dst, src):
+        def deal_words(dst, src):
             nc.vector.tensor_copy(
-                out=dst.rearrange("p e (a b m) -> p a e m b", a=2, b=2),
-                in_=src.rearrange("p e (m a b) -> p a e m b", a=2, b=2),
+                out=dst.rearrange("p (a b m) -> p a m b", a=2, b=2),
+                in_=src.rearrange("p (m a b) -> p a m b", a=2, b=2),
+            )
+
+        def deal_narrow(dst, src, run):
+            nc.vector.tensor_copy(
+                out=dst.rearrange("p e (t c m) -> p e c t m", t=PACK, m=run),
+                in_=src.rearrange("p e (c m t) -> p e c t m", t=PACK, m=run),
             )
 
         w_w = {}
@@ -170,19 +176,19 @@ def tile_moe_elr_s_relu_kernel(tc, x_words, x_scales, w_words, w_scales, wa, wb_
 
         def deal_w(pair):
             dealt = sbuf("w_w%d" % pair, [P, 2, 2 * N], U8)
-            deal(dealt[:].bitcast(U16), w_raw[pair][:].bitcast(U16))
+            deal_narrow(dealt[:].bitcast(U16), w_raw[pair][:].bitcast(U16), 8)
             for k in range(2):
                 w_w[2 * pair + k] = dealt[:, k, :]
 
         def deal_scales(first, count):
             dealt = sbuf("s_dealt%d" % first, [P, count, N], U8)
-            deal(dealt[:], s_raw[:, first * N:(first + count) * N].rearrange("p (e c) -> p e c", e=count))
+            deal_narrow(dealt[:], s_raw[:, first * N:(first + count) * N].rearrange("p (e c) -> p e c", e=count), 16)
             for k in range(count):
                 s_dealt[first + k] = dealt[:, k, :]
 
         def deal_wb(e):
-            wb_w[e] = sbuf("wb_w%d" % e, [P, 1, N], I32)
-            deal(wb_w[e][:], wb_raw[e][:].rearrange("p (e c) -> p e c", e=1))
+            wb_w[e] = sbuf("wb_w%d" % e, [P, N], I32)
+            deal_words(wb_w[e][:], wb_raw[e][:])
 
         def quantise_h(e):
             h_w[e] = sbuf("h_w%d" % e, [P, C], U32, over={0: "w_raw0", 2: "s_raw"}.get(e))
@@ -212,7 +218,7 @@ def tile_moe_elr_s_relu_kernel(tc, x_words, x_scales, w_words, w_scales, wa, wb_
                     )
                     nc.tensor.matmul_mx(
                         out=acc[:, g, :],
-                        lhsT=wb_w[e][:, 0, span(t, P)].bitcast(FP8X4), lhsT_scale=s_dealt[e][WB_ROWS:P, span(t, P)],
+                        lhsT=wb_w[e][:, span(t, P)].bitcast(FP8X4), lhsT_scale=s_dealt[e][WB_ROWS:P, span(t, P)],
                         rhs=h_w[e][:, own].bitcast(FP8X4), rhs_scale=h_s[e][:, own],
                         start=False, stop=True,
                     )

@@ -24,8 +24,8 @@ BANK_SLOTS = 128
 BANKS = 4
 LINE = 4
 WINDOW = 1536
-WA_PARTS = (1, 1, 1, 2)
-VECTOR_GROUPS = ((24,), (64,), (96,), (32, 48))
+WA_PARTS = (2, 1, 1, 2)
+VECTOR_GROUPS = ((0, 0), (72,), (96,), (0, 40))
 WB_ROWS = 4
 
 
@@ -90,19 +90,21 @@ def tile_moe_elr_s_relu_kernel(tc, x_words, x_scales, w_words, w_scales, wa, wb_
 
         nc.sync.dma_start(out=x_w[:, 0:T], in_=x_words[0].rearrange("p t d -> p (t d)").bitcast(I32))
         nc.sync.dma_start(offsets[:], offs)
+        load_wa(0, 0)
         for r in range(QUADRANTS):
             nc.sync.dma_start(out=x_s[r:P:32, 0:T].bitcast(I32), in_=x_scales[0, r:16:4, :].bitcast(I32))
-        for e in range(E - 1):
-            load_wa(e, 0)
+        load_wa(0, 1)
+        load_wa(1, 0)
+        load_wa(2, 0)
         load_w(0)
-        load_wb(0)
         load_scales(w_scales, 0)
-        load_wa(E - 1, 0)
+        load_wa(3, 0)
+        load_wb(0)
         load_scales(wb_scales, WB_ROWS)
         load_wb(1)
-        load_wa(E - 1, 1)
-        load_wb(2)
+        load_wa(3, 1)
         load_w(1)
+        load_wb(2)
         load_wb(3)
 
         slot_w = sbuf("slot_w", [P, E * C], U32)
@@ -123,7 +125,8 @@ def tile_moe_elr_s_relu_kernel(tc, x_words, x_scales, w_words, w_scales, wa, wb_
                 src = wa_raw[(e, part)][:].rearrange("p j (m a b) -> p a m j b", a=2, b=2)
                 cut = groups - VECTOR_GROUPS[e][part]
                 nc.scalar.copy(out=dst[:, :, part * groups:part * groups + cut], in_=src[:, :, 0:cut])
-                nc.vector.tensor_copy(out=dst[:, :, part * groups + cut:(part + 1) * groups], in_=src[:, :, cut:groups])
+                if cut < groups:
+                    nc.vector.tensor_copy(out=dst[:, :, part * groups + cut:(part + 1) * groups], in_=src[:, :, cut:groups])
             wa_w = sbuf("wa_w%d" % e, [P, H], U32)
             wa_s = sbuf("wa_s%d" % e, [P, H], U8)
             nc.vector.quantize_mx(out=wa_w[:].bitcast(FP8X4), scales=wa_s[:], in_=wa_bf[:])
@@ -139,7 +142,7 @@ def tile_moe_elr_s_relu_kernel(tc, x_words, x_scales, w_words, w_scales, wa, wb_
                     )
 
         def empty_h(e):
-            h_bf[e] = sbuf("h_bf%d" % e, [P, PACK * C], BF16)
+            h_bf[e] = sbuf("h_bf%d" % e, [P, PACK * C], BF16, over="wa_raw%d_0" % (e + 1) if e < E - 1 else None)
             for b in banks:
                 nc.scalar.activation(
                     out=h_bf[e][:, span(b, PACK * BANK_SLOTS)].rearrange("p (u t) -> p u t", t=PACK),
@@ -191,7 +194,7 @@ def tile_moe_elr_s_relu_kernel(tc, x_words, x_scales, w_words, w_scales, wa, wb_
             deal_words(wb_w[e][:], wb_raw[e][:])
 
         def quantise_h(e):
-            h_w[e] = sbuf("h_w%d" % e, [P, C], U32, over={0: "w_raw0", 2: "s_raw"}.get(e))
+            h_w[e] = sbuf("h_w%d" % e, [P, C], U32, over={0: "w_raw0", 2: "wa_raw3_1"}.get(e))
             h_s[e] = sbuf("h_s%d" % e, [P, C], U8)
             width = BANK_SLOTS if e == E - 1 else C
             for piece in range(C // width):

@@ -119,14 +119,22 @@ def tile_moe_elr_s_relu_kernel(tc, x_words, x_scales, w_words, w_scales, wa, wb_
 
         def first_product(e):
             wa_bf = sbuf("wa_bf%d" % e, [P, PACK * H], BF16)
-            dst = wa_bf[:].rearrange("p (a b m j) -> p a m j b", a=2, b=2, j=PACK)
+            by_pairs = wa_bf[:].rearrange("p (a b m j) -> p a m j b", a=2, b=2, j=PACK)
+            by_lines = wa_bf[:].rearrange("p (t m j) -> p m j t", t=PACK, j=PACK)
             groups = P // WA_PARTS[e]
             for part in range(WA_PARTS[e]):
-                src = wa_raw[(e, part)][:].rearrange("p j (m a b) -> p a m j b", a=2, b=2)
+                raw = wa_raw[(e, part)][:]
+                first = part * groups
                 cut = groups - VECTOR_GROUPS[e][part]
-                nc.scalar.copy(out=dst[:, :, part * groups:part * groups + cut], in_=src[:, :, 0:cut])
+                nc.scalar.copy(
+                    out=by_pairs[:, :, first:first + cut],
+                    in_=raw.rearrange("p j (m a b) -> p a m j b", a=2, b=2)[:, :, 0:cut],
+                )
                 if cut < groups:
-                    nc.vector.tensor_copy(out=dst[:, :, part * groups + cut:(part + 1) * groups], in_=src[:, :, cut:groups])
+                    nc.vector.tensor_copy(
+                        out=by_lines[:, first + cut:first + groups],
+                        in_=raw.rearrange("p j (m t) -> p m j t", t=PACK)[:, cut:groups],
+                    )
             wa_w = sbuf("wa_w%d" % e, [P, H], U32)
             wa_s = sbuf("wa_s%d" % e, [P, H], U8)
             nc.vector.quantize_mx(out=wa_w[:].bitcast(FP8X4), scales=wa_s[:], in_=wa_bf[:])
@@ -158,8 +166,8 @@ def tile_moe_elr_s_relu_kernel(tc, x_words, x_scales, w_words, w_scales, wa, wb_
 
         def deal_words(dst, src):
             nc.vector.tensor_copy(
-                out=dst.rearrange("p (a b m) -> p a m b", a=2, b=2),
-                in_=src.rearrange("p (m a b) -> p a m b", a=2, b=2),
+                out=dst.rearrange("p (t m) -> p m t", t=PACK),
+                in_=src.rearrange("p (m t) -> p m t", t=PACK),
             )
 
         def deal_narrow(dst, src, run):

@@ -245,13 +245,13 @@ def tile_moe_elr_s_relu_kernel(tc, x_words, x_scales, w_words, w_scales, wa, wb_
             for b in banks:
                 acc = y_acc[(e, b)]
                 if e == E - 1:
+                    nc.scalar.copy(out=y_f[e][:, :, span(b, BANK_SLOTS)], in_=acc[:])
+                    nc.sync.dma_start(out=out_rows[:, :, span(e * len(banks) + b, BANK_SLOTS)], in_=y_f[e][:, :, span(b, BANK_SLOTS)])
                     if b == 1:
                         nc.scalar.copy(
                             out=y_bf[e][:, span(b, PACK * BANK_SLOTS)].rearrange("p (u t) -> p u t", t=PACK),
                             in_=acc[:].rearrange("p t u -> p u t"),
                         )
-                    nc.scalar.copy(out=y_f[e][:, :, span(b, BANK_SLOTS)], in_=acc[:])
-                    nc.sync.dma_start(out=out_rows[:, :, span(e * len(banks) + b, BANK_SLOTS)], in_=y_f[e][:, :, span(b, BANK_SLOTS)])
                 else:
                     nc.scalar.copy(out=y_f[e][:, span(b, 2), :].rearrange("p t c -> p (t c)"), in_=acc[:].rearrange("p g u -> p (g u)"))
                     if e != 1:
@@ -274,8 +274,8 @@ def tile_moe_elr_s_relu_kernel(tc, x_words, x_scales, w_words, w_scales, wa, wb_
                     scales=y_s[:, columns],
                     in_=y_bf[e][:, span(piece, PACK * width)],
                 )
-            if e != 2:
-                columns = slice(min(e, 2) * C, (e + 1) * C)
+            if e != 1:
+                columns = slice((1 if e == 2 else e) * C, (e + 1) * C)
                 nc.sync.dma_start(out=out_words[:, columns], in_=y_w[:, columns].bitcast(I32))
 
         for e in range(E):

@@ -25,7 +25,7 @@ BANKS = 4
 LINE = 4
 WINDOW = 1536
 WA_PARTS = (2, 1, 1, 2)
-VECTOR_GROUPS = ((0, 0), (72,), (96,), (0, 40))
+VECTOR_GROUPS = ((0, 0), (72,), (96,), (0, 64))
 WB_ROWS = 4
 
 
@@ -40,13 +40,13 @@ def tile_moe_elr_s_relu_kernel(tc, x_words, x_scales, w_words, w_scales, wa, wb_
         start = {}
         used = [0]
 
-        def sbuf(name, shape, dtype, over=None):
+        def sbuf(name, shape, dtype, over=None, room=0):
             if over is None:
                 start[name] = sum(used)
                 size = ITEM_BYTES[dtype]
                 for extent in shape[1:]:
                     size = size * extent
-                used.append(size)
+                used.append(max(size, room))
             else:
                 start[name] = start[over]
             return work.tile(shape, dtype, name=name, tag=name, align_bytes=64, offset=start[name])
@@ -126,10 +126,11 @@ def tile_moe_elr_s_relu_kernel(tc, x_words, x_scales, w_words, w_scales, wa, wb_
                 raw = wa_raw[(e, part)][:]
                 first = part * groups
                 cut = groups - VECTOR_GROUPS[e][part]
-                nc.scalar.copy(
-                    out=by_pairs[:, :, first:first + cut],
-                    in_=raw.rearrange("p j (m a b) -> p a m j b", a=2, b=2)[:, :, 0:cut],
-                )
+                if cut > 0:
+                    nc.scalar.copy(
+                        out=by_pairs[:, :, first:first + cut],
+                        in_=raw.rearrange("p j (m a b) -> p a m j b", a=2, b=2)[:, :, 0:cut],
+                    )
                 if cut < groups:
                     nc.vector.tensor_copy(
                         out=by_lines[:, first + cut:first + groups],
@@ -150,10 +151,16 @@ def tile_moe_elr_s_relu_kernel(tc, x_words, x_scales, w_words, w_scales, wa, wb_
                     )
 
         def empty_h(e):
-            h_bf[e] = sbuf("h_bf%d" % e, [P, PACK * C], BF16, over="wa_raw%d_0" % (e + 1) if e < E - 1 else None)
+            if e < E - 1:
+                whole = sbuf("h_bf%d" % e, [P, PACK * C], BF16, over="wa_raw%d_0" % (e + 1))
+                h_bf[e] = [whole[:]]
+                parts = [whole[:, span(b, PACK * BANK_SLOTS)] for b in banks]
+            else:
+                parts = [sbuf("h_bf%d_%d" % (e, b), [P, PACK * BANK_SLOTS], BF16, room=2 * PACK * C)[:] for b in banks]
+                h_bf[e] = parts
             for b in banks:
                 nc.scalar.activation(
-                    out=h_bf[e][:, span(b, PACK * BANK_SLOTS)].rearrange("p (u t) -> p u t", t=PACK),
+                    out=parts[b].rearrange("p (u t) -> p u t", t=PACK),
                     in_=h_acc[(e, b)][:].rearrange("p t u -> p u t"),
                     func=RELU,
                 )
@@ -209,7 +216,7 @@ def tile_moe_elr_s_relu_kernel(tc, x_words, x_scales, w_words, w_scales, wa, wb_
                 nc.vector.quantize_mx(
                     out=h_w[e][:, span(piece, width)].bitcast(FP8X4),
                     scales=h_s[e][:, span(piece, width)],
-                    in_=h_bf[e][:, span(piece, PACK * width)],
+                    in_=h_bf[e][piece],
                 )
 
         def second_product(e):
@@ -241,7 +248,7 @@ def tile_moe_elr_s_relu_kernel(tc, x_words, x_scales, w_words, w_scales, wa, wb_
 
         def empty_y(e):
             y_f[e] = sbuf("y_f%d" % e, [P, PACK, C], F32)
-            y_bf[e] = sbuf("y_bf%d" % e, [P, PACK * C], BF16, over="h_bf3" if e == 1 else None)
+            y_bf[e] = sbuf("y_bf%d" % e, [P, PACK * C], BF16, over="h_bf3_0" if e == 1 else None)
             for b in banks:
                 acc = y_acc[(e, b)]
                 if e == E - 1:

from contextlib import ExitStack

import concourse.mybir as mybir

K, T, E, C, H, N = 512, 512, 4, 256, 512, 512
FLOPS = 2 * E * C * (K * H + K * N + H * N)

F32 = mybir.dt.float32
BF16 = mybir.dt.bfloat16
I32 = mybir.dt.int32
U32 = mybir.dt.uint32
U16 = mybir.dt.uint16
U8 = mybir.dt.uint8
FP8X4 = mybir.dt.float8_e4m3fn_x4
FP4X4 = mybir.dt.float4_e2m1fn_x4
RELU = mybir.ActivationFunctionType.Relu

ITEM_BYTES = {F32: 4, BF16: 2, I32: 4, U32: 4, U8: 1}

P = 128
PACK = 4
QUADRANTS = 4
BANK_SLOTS = 128
BANKS = 4
LINE = 4
WINDOW = 1536
WA_PARTS = (2, 1, 1, 2)
VECTOR_GROUPS = ((0, 0), (72,), (96,), (0, 64))
WB_ROWS = 4


def tile_moe_elr_s_relu_kernel(tc, x_words, x_scales, w_words, w_scales, wa, wb_words, wb_scales, offs, out_0, out_1, out_2):
    nc = tc.nc
    with ExitStack() as ctx:
        keep = ctx.enter_context(tc.tile_pool(name="keep", bufs=1))
        work = ctx.enter_context(tc.tile_pool(name="work", bufs=1))
        psum_h = ctx.enter_context(tc.psum_pool(name="psum_h", bufs=BANKS))
        psum_y = ctx.enter_context(tc.psum_pool(name="psum_y", bufs=BANKS))

        start = {}
        used = [0]

        def sbuf(name, shape, dtype, over=None, room=0):
            if over is None:
                start[name] = sum(used)
                size = ITEM_BYTES[dtype]
                for extent in shape[1:]:
                    size = size * extent
                used.append(max(size, room))
            else:
                start[name] = start[over]
            return work.tile(shape, dtype, name=name, tag=name, align_bytes=64, offset=start[name])

        def span(index, width):
            return slice(index * width, (index + 1) * width)

        offsets = keep.tile([P, E * C // 16], U16, name="offsets")
        x_w = sbuf("x_w", [P, WINDOW], I32)
        x_s = sbuf("x_s", [P, WINDOW], U8)
        s_raw = sbuf("s_raw", [P, E * N], U8)
        nc.vector.memset(x_s[:, 0:T].bitcast(I32), 0)
        nc.vector.memset(s_raw[:].bitcast(I32), 0)
        nc.vector.memset(x_w[:, T:WINDOW], 0)
        nc.vector.memset(x_s[:, T:WINDOW].bitcast(I32), 0)

        wa_raw = {}
        w_raw = {}
        wb_raw = {}

        def load_wa(e, part):
            width = H // WA_PARTS[e]
            rows = wa[e].rearrange("(p j) c -> p j c", j=PACK)
            wa_raw[(e, part)] = sbuf("wa_raw%d_%d" % (e, part), [P, PACK, width], F32)
            nc.sync.dma_start(out=wa_raw[(e, part)][:], in_=rows[:, :, span(part, width)])

        def load_w(pair):
            w_raw[pair] = sbuf("w_raw%d" % pair, [P, 2, N // 2], I32)
            nc.sync.dma_start(out=w_raw[pair][:], in_=w_words[span(pair, 2), 0].bitcast(I32).rearrange("e p c -> p e c"))

        def load_wb(e):
            wb_raw[e] = sbuf("wb_raw%d" % e, [P, N], I32)
            nc.sync.dma_start(out=wb_raw[e][:], in_=wb_words[e, 0].rearrange("p n d -> p (n d)").bitcast(I32))

        def load_scales(scales, first):
            for r in range(QUADRANTS):
                nc.sync.dma_start(
                    out=s_raw[first + r:P:32, :].bitcast(I32).rearrange("q (e c) -> q e c", e=E),
                    in_=scales[:, 0, r:16:4, :].bitcast(I32).rearrange("e q c -> q e c"),
                )

        nc.sync.dma_start(out=x_w[:, 0:T], in_=x_words[0].rearrange("p t d -> p (t d)").bitcast(I32))
        nc.sync.dma_start(offsets[:], offs)
        load_wa(0, 0)
        for r in range(QUADRANTS):
            nc.sync.dma_start(out=x_s[r:P:32, 0:T].bitcast(I32), in_=x_scales[0, r:16:4, :].bitcast(I32))
        load_wa(0, 1)
        load_wa(1, 0)
        load_wa(2, 0)
        load_w(0)
        load_scales(w_scales, 0)
        load_wa(3, 0)
        load_wb(0)
        load_scales(wb_scales, WB_ROWS)
        load_wb(1)
        load_wa(3, 1)
        load_w(1)
        load_wb(2)
        load_wb(3)

        slot_w = sbuf("slot_w", [P, E * C], U32)
        slot_s = sbuf("slot_s", [P, E * C], U8)
        nc.vector.tensor_copy(slot_w[:], x_w[:].bitcast(U32).indirect(offsets[:]))
        nc.vector.tensor_copy(slot_s[:], x_s[:].indirect(offsets[:]))

        banks = range(C // BANK_SLOTS)

        h_acc = {}
        h_bf = {}

        def first_product(e):
            wa_bf = sbuf("wa_bf%d" % e, [P, PACK * H], BF16)
            by_pairs = wa_bf[:].rearrange("p (a b m j) -> p a m j b", a=2, b=2, j=PACK)
            by_lines = wa_bf[:].rearrange("p (t m j) -> p m j t", t=PACK, j=PACK)
            groups = P // WA_PARTS[e]
            for part in range(WA_PARTS[e]):
                raw = wa_raw[(e, part)][:]
                first = part * groups
                cut = groups - VECTOR_GROUPS[e][part]
                if cut > 0:
                    nc.scalar.copy(
                        out=by_pairs[:, :, first:first + cut],
                        in_=raw.rearrange("p j (m a b) -> p a m j b", a=2, b=2)[:, :, 0:cut],
                    )
                if cut < groups:
                    nc.vector.tensor_copy(
                        out=by_lines[:, first + cut:first + groups],
                        in_=raw.rearrange("p j (m t) -> p m j t", t=PACK)[:, cut:groups],
                    )
            wa_w = sbuf("wa_w%d" % e, [P, H], U32)
            wa_s = sbuf("wa_s%d" % e, [P, H], U8)
            nc.vector.quantize_mx(out=wa_w[:].bitcast(FP8X4), scales=wa_s[:], in_=wa_bf[:])
            for b in banks:
                slots = span(e * len(banks) + b, BANK_SLOTS)
                h_acc[(e, b)] = psum_h.tile([P, PACK, BANK_SLOTS], F32, name="acc_h")
                for t in range(PACK):
                    nc.tensor.matmul_mx(
                        out=h_acc[(e, b)][:, t, :],
                        lhsT=wa_w[:, span(t, P)].bitcast(FP8X4), lhsT_scale=wa_s[:, span(t, P)],
                        rhs=slot_w[:, slots].bitcast(FP8X4), rhs_scale=slot_s[:, slots],
                        start=True, stop=True,
                    )

        def empty_h(e):
            if e < E - 1:
                whole = sbuf("h_bf%d" % e, [P, PACK * C], BF16, over="wa_raw%d_0" % (e + 1))
                h_bf[e] = [whole[:]]
                parts = [whole[:, span(b, PACK * BANK_SLOTS)] for b in banks]
            else:
                parts = [sbuf("h_bf%d_%d" % (e, b), [P, PACK * BANK_SLOTS], BF16, room=2 * PACK * C)[:] for b in banks]
                h_bf[e] = parts
            for b in banks:
                nc.scalar.activation(
                    out=parts[b].rearrange("p (u t) -> p u t", t=PACK),
                    in_=h_acc[(e, b)][:].rearrange("p t u -> p u t"),
                    func=RELU,
                )

        for e in range(E):
            first_product(e)
            if e > 0:
                empty_h(e - 1)
        empty_h(E - 1)

        def deal_words(dst, src):
            nc.vector.tensor_copy(
                out=dst.rearrange("p (t m) -> p m t", t=PACK),
                in_=src.rearrange("p (m t) -> p m t", t=PACK),
            )

        def deal_narrow(dst, src, run):
            nc.vector.tensor_copy(
                out=dst.rearrange("p e (t c m) -> p e c t m", t=PACK, m=run),
                in_=src.rearrange("p e (c m t) -> p e c t m", t=PACK, m=run),
            )

        w_w = {}
        wb_w = {}
        s_dealt = {}
        h_w = {}
        h_s = {}
        y_acc = {}
        y_f = {}
        y_bf = {}

        def deal_w(pair):
            dealt = sbuf("w_w%d" % pair, [P, 2, 2 * N], U8)
            deal_narrow(dealt[:].bitcast(U16), w_raw[pair][:].bitcast(U16), 8)
            for k in range(2):
                w_w[2 * pair + k] = dealt[:, k, :]

        def deal_scales(first, count):
            dealt = sbuf("s_dealt%d" % first, [P, count, N], U8)
            deal_narrow(dealt[:], s_raw[:, first * N:(first + count) * N].rearrange("p (e c) -> p e c", e=count), 16)
            for k in range(count):
                s_dealt[first + k] = dealt[:, k, :]

        def deal_wb(e):
            wb_w[e] = sbuf("wb_w%d" % e, [P, N], I32)
            deal_words(wb_w[e][:], wb_raw[e][:])

        def quantise_h(e):
            h_w[e] = sbuf("h_w%d" % e, [P, C], U32, over={0: "w_raw0", 2: "wa_raw3_1"}.get(e))
            h_s[e] = sbuf("h_s%d" % e, [P, C], U8)
            width = BANK_SLOTS if e == E - 1 else C
            for piece in range(C // width):
                nc.vector.quantize_mx(
                    out=h_w[e][:, span(piece, width)].bitcast(FP8X4),
                    scales=h_s[e][:, span(piece, width)],
                    in_=h_bf[e][piece],
                )

        def second_product(e):
            last = e == E - 1
            for b in banks:
                acc = psum_y.tile([P, PACK, BANK_SLOTS], F32, name="acc_y")
                y_acc[(e, b)] = acc
                for g in range(PACK):
                    t, half = (g, b) if last else (2 * b + g // 2, g % 2)
                    own = span(half, BANK_SLOTS)
                    slots = span(e * len(banks) + half, BANK_SLOTS)
                    nc.tensor.matmul_mx(
                        out=acc[:, g, :],
                        lhsT=w_w[e][:, span(t, 2 * P)].bitcast(FP4X4), lhsT_scale=s_dealt[e][:, span(t, P)],
                        rhs=slot_w[:, slots].bitcast(FP8X4), rhs_scale=slot_s[:, slots],
                        start=True, stop=False,
                    )
                    nc.tensor.matmul_mx(
                        out=acc[:, g, :],
                        lhsT=wb_w[e][:, span(t, P)].bitcast(FP8X4), lhsT_scale=s_dealt[e][WB_ROWS:P, span(t, P)],
                        rhs=h_w[e][:, own].bitcast(FP8X4), rhs_scale=h_s[e][:, own],
                        start=False, stop=True,
                    )

        out_rows = out_0.rearrange("(p t) j -> p t j", t=PACK)
        out_words = out_1[0].rearrange("p j d -> p (j d)").bitcast(I32)
        y_w = sbuf("y_w", [P, E * C], U32)
        y_s = sbuf("y_s", [P, E * C], U8)

        def empty_y(e):
            y_f[e] = sbuf("y_f%d" % e, [P, PACK, C], F32)
            y_bf[e] = sbuf("y_bf%d" % e, [P, PACK * C], BF16, over="h_bf3_0" if e == 1 else None)
            for b in banks:
                acc = y_acc[(e, b)]
                if e == E - 1:
                    nc.scalar.copy(out=y_f[e][:, :, span(b, BANK_SLOTS)], in_=acc[:])
                    nc.sync.dma_start(out=out_rows[:, :, span(e * len(banks) + b, BANK_SLOTS)], in_=y_f[e][:, :, span(b, BANK_SLOTS)])
                    if b == 1:
                        nc.scalar.copy(
                            out=y_bf[e][:, span(b, PACK * BANK_SLOTS)].rearrange("p (u t) -> p u t", t=PACK),
                            in_=acc[:].rearrange("p t u -> p u t"),
                        )
                else:
                    nc.scalar.copy(out=y_f[e][:, span(b, 2), :].rearrange("p t c -> p (t c)"), in_=acc[:].rearrange("p g u -> p (g u)"))
                    if e != 1:
                        nc.sync.dma_start(out=out_rows[:, span(b, 2), span(e, C)], in_=y_f[e][:, span(b, 2), :])
            if e == 1:
                nc.sync.dma_start(out=out_rows[:, :, span(e, C)], in_=y_f[e][:])

        def round_y(e, width):
            nc.vector.tensor_copy(
                out=y_bf[e][:, 0:PACK * width].rearrange("p (c i t) -> p c t i", i=LINE, t=PACK),
                in_=y_f[e][:, :, 0:width].rearrange("p t (c i) -> p c t i", i=LINE),
            )

        def quantise_y(e):
            width = BANK_SLOTS if e == E - 1 else C
            for piece in range(C // width):
                columns = slice(e * C + piece * width, e * C + (piece + 1) * width)
                nc.vector.quantize_mx(
                    out=y_w[:, columns].bitcast(FP8X4),
                    scales=y_s[:, columns],
                    in_=y_bf[e][:, span(piece, PACK * width)],
                )
            if e != 1:
                columns = slice((1 if e == 2 else e) * C, (e + 1) * C)
                nc.sync.dma_start(out=out_words[:, columns], in_=y_w[:, columns].bitcast(I32))

        for e in range(E):
            if e % 2 == 0:
                deal_w(e // 2)
            if e < 3:
                deal_scales(e, 1 if e < 2 else 2)
            deal_wb(e)
            quantise_h(e)
            if e >= 2:
                empty_y(e - 2)
            second_product(e)
        empty_y(E - 2)
        empty_y(E - 1)
        for e in range(E):
            round_y(e, BANK_SLOTS if e == E - 1 else C)
            if e > 0:
                quantise_y(e - 1)
        quantise_y(E - 1)

        for r in range(QUADRANTS):
            nc.scalar.dma_start(out=out_2[0, r:16:4, :].bitcast(I32), in_=y_s[r:P:32, :].bitcast(I32))
